import numpy as np
import ml_dtypes


def mxq(x, axis, fmt="e4m3"):
    dtype, down = {"e4m3": (ml_dtypes.float8_e4m3fn, 7), "e5m2": (ml_dtypes.float8_e5m2, 14)}[fmt]
    v = np.moveaxis(np.asarray(x, np.float32).astype(ml_dtypes.bfloat16).astype(np.float64), axis, -1)
    blocks = v.reshape(v.shape[:-1] + (-1, 32))
    amax = np.abs(blocks).max(-1, keepdims=True)
    byte = np.maximum(np.where(amax > 0, np.frexp(amax)[1] - 1 + 127, 0) - down, 1)
    scale = np.exp2(byte - 127.0)
    codes = (blocks / scale).astype(np.float32).astype(dtype).astype(np.float64)
    return np.moveaxis((codes * scale).reshape(v.shape), -1, axis)


WIDE = False


def mx_kscale(k):
    if not WIDE:
        return np.ones(k)
    levels = np.array([10, -10, 5, -5, 0])
    if k % 512:
        return np.exp2(np.random.permutation(np.resize(levels, k // 32))).repeat(32)
    a = np.empty((k // 512, 16))
    for p in range(k // 512):
        a[p, :8] = np.random.permutation(np.resize(levels, 8))
        for g in range(8):
            far = levels[np.abs(levels - a[p, g]) >= 10]
            a[p, g + 8] = far[np.random.randint(len(far))]
    return np.exp2(a.ravel()).repeat(32)


def f64(x):
    return np.asarray(x).astype(np.float64)


def striped(idx):
    return np.tile(idx.reshape(-1, 16).T, (8, 1)).astype(np.uint16)


def unstriped(offs):
    return offs[:16].T.reshape(-1).astype(np.int64)


def pack_weight(w):
    k, n = w.shape
    w = f64(np.asarray(w, np.float32).astype(ml_dtypes.bfloat16)).reshape(k // 32, 32, n)
    amax = np.abs(w).max(1)
    byte = np.clip(np.where(amax > 0, np.frexp(amax)[1] - 1 + 127 - 7, 1), 1, 254)
    scaled = (w * np.exp2(127.0 - byte)[:, None, :]).reshape(k, n).astype(np.float32)
    words = np.ascontiguousarray(scaled.reshape(k // 512, 128, 4, n).transpose(0, 1, 3, 2)).astype(ml_dtypes.float8_e4m3fn).view(np.uint8)
    return words, np.ascontiguousarray(byte.astype(np.uint8).reshape(k // 512, 16, n))


def unpack_weight(words, scales):
    g, p, n, _ = words.shape
    vals = np.ascontiguousarray(words).view(ml_dtypes.float8_e4m3fn).astype(np.float64) * np.repeat(np.exp2(scales.astype(np.float64) - 127.0), 8, axis=1)[..., None]
    return vals.transpose(0, 1, 3, 2).reshape(g * 512, n)


K, T, S, N, V = 1024, 1024, 512, 256, 256
P = 2 ** 7


def setup_inputs():
    n = np.random.standard_normal
    s = mx_kscale(K)[:, None]
    packed_xT = pack_weight(n((K, T)) * s)
    return {
        "x_words": packed_xT[0],
        "x_scales": packed_xT[1],
        "w1": (n((K, N)) / np.sqrt(K) / s).astype(np.float32),
        "w2": (n((K, N)) / np.sqrt(K) / s).astype(np.float32),
        "w3": (n((K, N)) / np.sqrt(K) / s).astype(np.float32),
        "sn": (np.tile(np.where(np.random.uniform(size=S) < 0.5, 1.0, -1.0), (P, 1))).astype(np.float32),
        "sa": (np.tile(np.where(np.random.uniform(size=V) < 0.5, 1.0, -1.0), (P, 1))).astype(np.float32),
        "sb": (np.tile(np.where(np.random.uniform(size=V) < 0.5, 1.0, -1.0), (P, 1))).astype(np.float32),
        "sf": (np.tile(np.where(np.random.uniform(size=S) < 0.5, 1.0, -1.0), (P, 1))).astype(np.float32),
        "offs": striped(np.random.permutation(T)[:S]),
        "inc": striped(np.random.permutation(S)),
        "head": striped(np.random.permutation(np.concatenate([np.arange(V), np.random.randint(0, V, S - V)]))),
        "tail": striped(np.random.permutation(np.concatenate([np.arange(V), np.random.randint(0, V, S - V)]))),
        "tri": striped(np.random.permutation(S)[:V]),
        "trj": striped(np.random.permutation(S)[:V]),
        "face": striped(np.random.permutation(np.concatenate([np.arange(V), np.random.randint(0, V, S - V)]))),
    }


def reference(x_words, x_scales, w1, w2, w3, sn, sa, sb, sf, offs, inc, head, tail, tri, trj, face):
    xq = unpack_weight(x_words, x_scales)[:, unstriped(offs)]
    own = mxq(f64(w3), 0, "e4m3").T @ xq
    y = mxq(f64(w1), 0, "e4m3").T @ xq
    li = y[:, unstriped(inc)] * f64(sn)[:1]
    dv = li.reshape(len(li), -1, 2).sum(axis=2)
    down = dv[:, unstriped(head)] - dv[:, unstriped(tail)]
    h = mxq(f64(w2), 0, "e4m3").T @ xq
    cu = h[:, unstriped(tri)] * f64(sa)[:1] + h[:, unstriped(trj)] * f64(sb)[:1]
    up = cu[:, unstriped(face)] * f64(sf)[:1]
    return np.tanh(own + down + up)

@@ -1,0 +1,194 @@
+from contextlib import ExitStack
+
+import concourse.mybir as mybir
+
+K, T, S, N, V = 1024, 1024, 512, 256, 256
+P = 128
+PACK = 4
+K_PASS = P * PACK
+PASSES = K // K_PASS
+BLOCKS = N // P
+HALF = S // 2
+SPARE = 16
+SCALE_ROWS = 4
+FLOPS = 3 * 2 * K * N * S
+
+F32 = mybir.dt.float32
+BF16 = mybir.dt.bfloat16
+I32 = mybir.dt.int32
+U32 = mybir.dt.uint32
+U16 = mybir.dt.uint16
+U8 = mybir.dt.uint8
+FP8X4 = mybir.dt.float8_e4m3fn_x4
+ADD = mybir.AluOpType.add
+SUB = mybir.AluOpType.subtract
+MULT = mybir.AluOpType.mult
+TANH = mybir.ActivationFunctionType.Tanh
+
+
+def tile_picked_yhodge_tanh_p_kernel(
+    tc, x_words, x_scales, w1, w2, w3, sn, sa, sb, sf, offs, inc, head, tail, tri, trj, face, out
+):
+    nc = tc.nc
+    with ExitStack() as ctx:
+        keep = ctx.enter_context(tc.tile_pool(name="keep", bufs=1))
+        psum = ctx.enter_context(tc.psum_pool(name="psum", bufs=1))
+
+        def sbuf(name, shape, dtype):
+            return keep.tile(shape, dtype, name=name, align_bytes=64)
+
+        def load(name, src, dtype):
+            t = sbuf(name, list(src.shape), dtype)
+            nc.sync.dma_start(t[:], src)
+            return t
+
+        def load_words(o):
+            t = sbuf("x_all%d" % o, [P, T], U32)
+            nc.sync.dma_start(t[:].bitcast(I32), x_words[o].rearrange("p c r -> p (c r)").bitcast(I32))
+            return t
+
+        def load_weight(name, w, o):
+            t = sbuf("%s_raw%d" % (name, o), [P, PACK, N], F32)
+            nc.sync.dma_start(t[:], w[o * K_PASS : (o + 1) * K_PASS, :].rearrange("(p t) c -> p t c", t=PACK))
+            return t
+
+        scale_all = sbuf("scale_all", [P, T], U8)
+        nc.vector.memset(scale_all[:].bitcast(I32), 0)
+        zeros = sbuf("zeros", [P, SPARE], F32)
+        nc.vector.memset(zeros[:], 0.0)
+        y_win = [sbuf("y_win%d" % b, [P, S + SPARE], F32) for b in range(BLOCKS)]
+        h_win = [sbuf("h_win%d" % b, [P, S], F32) for b in range(BLOCKS)]
+        dv_win = [sbuf("dv_win%d" % b, [P, 2 * S], F32) for b in range(BLOCKS)]
+        cu_win = [sbuf("cu_win%d" % b, [P, S + SPARE], F32) for b in range(BLOCKS)]
+
+        offs_t = load("offs_t", offs, U16)
+        x_all = [load_words(o) for o in range(PASSES)]
+        for q in range(4):
+            nc.scalar.dma_start(
+                scale_all[32 * q : 32 * q + PASSES * SCALE_ROWS, :].bitcast(I32),
+                x_scales[:, SCALE_ROWS * q : SCALE_ROWS * (q + 1), :].bitcast(I32),
+            )
+        for b in range(BLOCKS):
+            nc.scalar.activation(y_win[b][:, S:], zeros[:], TANH)
+            nc.vector.memset(dv_win[b][:, V:], 0.0)
+            nc.vector.memset(cu_win[b][:, V:], 0.0)
+        w1_raw = [load_weight("w1", w1, o) for o in range(PASSES)]
+        inc_t = load("inc_t", inc, U16)
+        sn_t = load("sn_t", sn, F32)
+        w2_raw = [load_weight("w2", w2, o) for o in range(PASSES)]
+        tri_t = load("tri_t", tri, U16)
+        trj_t = load("trj_t", trj, U16)
+        sa_t = load("sa_t", sa, F32)
+        sb_t = load("sb_t", sb, F32)
+        face_t = load("face_t", face, U16)
+        head_t = load("head_t", head, U16)
+        tail_t = load("tail_t", tail, U16)
+        sf_t = load("sf_t", sf, F32)
+        w3_raw = [load_weight("w3", w3, o) for o in range(PASSES)]
+
+        x_pick = [sbuf("x_pick%d" % o, [P, S], U32) for o in range(PASSES)]
+        scale_pick = sbuf("scale_pick", [P, S], U8)
+        nc.vector.tensor_copy(x_pick[0][:], x_all[0][:].indirect(offs_t[:]))
+        nc.vector.tensor_copy(x_pick[1][:], x_all[1][:].indirect(offs_t[:]))
+        nc.vector.tensor_copy(scale_pick[:], scale_all[:].indirect(offs_t[:]))
+
+        def interleave(name, raw, c0, width, copy):
+            t = sbuf(name, [P, width, PACK], BF16)
+            copy(
+                t[:].rearrange("p (c i) t -> p c t i", i=4),
+                raw[:, :, c0 : c0 + width].rearrange("p t (c i) -> p c t i", i=4),
+            )
+            return t
+
+        def quantize(name, grouped, width):
+            codes = sbuf(name + "_codes", [P, width], U32)
+            scales = sbuf(name + "_scales", [P, width], U8)
+            nc.vector.quantize_mx(
+                out=codes[:].bitcast(FP8X4), scales=scales[:], in_=grouped[:].rearrange("p c t -> p (c t)")
+            )
+            return codes, scales
+
+        def project(name, wq, c0, n0, n1):
+            acc = psum.tile([P, n1 - n0], F32, name=name)
+            for o in range(PASSES):
+                codes, scales = wq[o]
+                nc.tensor.matmul_mx(
+                    out=acc[:],
+                    lhsT=codes[:, c0 : c0 + P].bitcast(FP8X4),
+                    lhsT_scale=scales[:, c0 : c0 + P],
+                    rhs=x_pick[o][:, n0:n1].bitcast(FP8X4),
+                    rhs_scale=scale_pick[SCALE_ROWS * o :, n0:n1],
+                    start=(o == 0),
+                    stop=(o == PASSES - 1),
+                )
+            return acc
+
+        g00 = interleave("g1_00", w1_raw[0], 0, P, nc.scalar.copy)
+        q00 = quantize("q1_00", g00, P)
+        g01 = interleave("g1_01", w1_raw[0], P, P, nc.scalar.copy)
+        g10 = interleave("g1_10", w1_raw[1], 0, P, nc.vector.tensor_copy)
+        q01 = quantize("q1_01", g01, P)
+        q10 = quantize("q1_10", g10, P)
+        g11 = interleave("g1_11", w1_raw[1], P, P, nc.scalar.copy)
+        ya = project("y0a", [q00, q10], 0, 0, HALF)
+        yb = project("y0b", [q00, q10], 0, HALF, S)
+        q11 = quantize("q1_11", g11, P)
+        nc.vector.tensor_copy(y_win[0][:, 0:HALF], ya[:])
+        nc.scalar.copy(y_win[0][:, HALF:S], yb[:])
+        y1 = project("y1", [q01, q11], 0, 0, S)
+        nc.scalar.copy(y_win[1][:, 0:S], y1[:])
+
+        g2 = [interleave("g2_%d" % o, w2_raw[o], 0, N, nc.scalar.copy) for o in range(PASSES)]
+        li = [sbuf("li%d" % b, [P, S], F32) for b in range(BLOCKS)]
+        nc.vector.tensor_tensor(li[0][:], y_win[0][:].indirect(inc_t[:]), sn_t[:], MULT)
+        q2 = [quantize("q2_0", g2[0], N)]
+        nc.vector.tensor_tensor(li[1][:], y_win[1][:].indirect(inc_t[:]), sn_t[:], MULT)
+        q2.append(quantize("q2_1", g2[1], N))
+        for b in range(BLOCKS):
+            acc = project("h%d" % b, q2, b * P, 0, S)
+            nc.scalar.copy(h_win[b][:], acc[:])
+        for b in range(BLOCKS):
+            pairs = li[b][:].rearrange("p (v d) -> p d v", d=2)
+            nc.vector.tensor_tensor(dv_win[b][:, 0:V], pairs[:, 0, :], pairs[:, 1, :], ADD)
+
+        g3 = [interleave("g3_%d" % o, w3_raw[o], 0, N, nc.scalar.copy) for o in range(PASSES)]
+        ca = [sbuf("ca%d" % b, [P, V], F32) for b in range(BLOCKS)]
+        cb = [sbuf("cb%d" % b, [P, V], F32) for b in range(BLOCKS)]
+        for b in range(BLOCKS):
+            nc.vector.tensor_tensor(ca[b][:], h_win[b][:].indirect(tri_t[:]), sa_t[:], MULT)
+            nc.vector.tensor_tensor(cb[b][:], h_win[b][:].indirect(trj_t[:]), sb_t[:], MULT)
+        q3 = []
+        for b in range(BLOCKS):
+            nc.vector.tensor_tensor(cu_win[b][:, 0:V], ca[b][:], cb[b][:], ADD)
+            q3.append(quantize("q3_%d" % b, g3[b], N))
+        own = [project("own%d" % b, q3, b * P, 0, S) for b in range(BLOCKS)]
+
+        def cols(lst, e0, e1):
+            return lst[:, e0 // 16 : e1 // 16]
+
+        pieces = [(0, 0, S), (1, 0, HALF), (1, HALF, S)]
+        up, t1, t2 = {}, {}, {}
+
+        def stage(i, k):
+            b, e0, e1 = pieces[i]
+            n = e1 - e0
+            if k == 0:
+                up[i] = sbuf("up%d" % i, [P, n], F32)
+                nc.vector.tensor_tensor(up[i][:], cu_win[b][:].indirect(cols(face_t, e0, e1)), sf_t[:, e0:e1], MULT)
+            elif k == 1:
+                t1[i] = sbuf("t1_%d" % i, [P, n], F32)
+                nc.vector.tensor_tensor(t1[i][:], dv_win[b][:].indirect(cols(head_t, e0, e1)), up[i][:], ADD)
+            elif k == 2:
+                t2[i] = sbuf("t2_%d" % i, [P, n], F32)
+                nc.vector.tensor_tensor(t2[i][:], dv_win[b][:].indirect(cols(tail_t, e0, e1)), t1[i][:], SUB)
+            else:
+                pre = sbuf("pre%d" % i, [P, n], F32)
+                nc.vector.tensor_tensor(pre[:], own[b][:, e0:e1], t2[i][:], SUB)
+                res = sbuf("res%d" % i, [P, n], F32)
+                nc.scalar.activation(res[:], pre[:], TANH)
+                nc.sync.dma_start(out[b * P : (b + 1) * P, e0:e1], res[:])
+
+        for step in range(len(pieces) + 3):
+            for i in range(len(pieces)):
+                if 0 <= step - i < 4:
+                    stage(i, step - i)

@@ -1,6 +1,7 @@
 from contextlib import ExitStack
 
 import concourse.mybir as mybir
+from concourse.masks import make_identity
 
 K, T, S, N, V = 1024, 1024, 512, 256, 256
 P = 128
@@ -34,8 +35,11 @@ def tile_picked_yhodge_tanh_p_kernel(
         keep = ctx.enter_context(tc.tile_pool(name="keep", bufs=1))
         psum = ctx.enter_context(tc.psum_pool(name="psum", bufs=1))
 
-        def sbuf(name, shape, dtype):
-            return keep.tile(shape, dtype, name=name, align_bytes=64)
+        def sbuf(name, shape, dtype, tag=None):
+            return keep.tile(shape, dtype, name=name, tag=tag or name, align_bytes=64)
+
+        def bank(name, i, width):
+            return psum.tile([P, width], F32, name=name, tag="bank%d" % i)
 
         def load(name, src, dtype):
             t = sbuf(name, list(src.shape), dtype)
@@ -47,22 +51,25 @@ def tile_picked_yhodge_tanh_p_kernel(
             nc.sync.dma_start(t[:].bitcast(I32), x_words[o].rearrange("p c r -> p (c r)").bitcast(I32))
             return t
 
-        def load_weight(name, w, o):
-            t = sbuf("%s_raw%d" % (name, o), [P, PACK, N], F32)
-            nc.sync.dma_start(t[:], w[o * K_PASS : (o + 1) * K_PASS, :].rearrange("(p t) c -> p t c", t=PACK))
+        def load_weight(name, w, o, c0=0, width=N):
+            t = sbuf("%s_raw%d_%d" % (name, o, c0), [P, PACK, width], F32)
+            rows = w[o * K_PASS : (o + 1) * K_PASS, c0 : c0 + width]
+            nc.sync.dma_start(t[:], rows.rearrange("(p t) c -> p t c", t=PACK))
             return t
 
         scale_all = sbuf("scale_all", [P, T], U8)
-        nc.vector.memset(scale_all[:].bitcast(I32), 0)
+        nc.gpsimd.memset(scale_all[:].bitcast(I32), 0)
         zeros = sbuf("zeros", [P, SPARE], F32)
         nc.vector.memset(zeros[:], 0.0)
         y_win = [sbuf("y_win%d" % b, [P, S + SPARE], F32) for b in range(BLOCKS)]
         h_win = [sbuf("h_win%d" % b, [P, S], F32) for b in range(BLOCKS)]
         dv_win = [sbuf("dv_win%d" % b, [P, 2 * S], F32) for b in range(BLOCKS)]
+        ident = sbuf("ident", [P, P], F32)
+        make_identity(nc, ident[:])
         cu_win = [sbuf("cu_win%d" % b, [P, S + SPARE], F32) for b in range(BLOCKS)]
 
         offs_t = load("offs_t", offs, U16)
-        x_all = [load_words(o) for o in range(PASSES)]
+        x_all = [load_words(0)]
         for q in range(4):
             nc.scalar.dma_start(
                 scale_all[32 * q : 32 * q + PASSES * SCALE_ROWS, :].bitcast(I32),
@@ -72,123 +79,172 @@ def tile_picked_yhodge_tanh_p_kernel(
             nc.scalar.activation(y_win[b][:, S:], zeros[:], TANH)
             nc.vector.memset(dv_win[b][:, V:], 0.0)
             nc.vector.memset(cu_win[b][:, V:], 0.0)
-        w1_raw = [load_weight("w1", w1, o) for o in range(PASSES)]
+        w1_raw = {(0, 0): load_weight("w1", w1, 0, 0, P)}
+        x_all.append(load_words(1))
+        w1_raw[1, 0] = load_weight("w1", w1, 1, 0, P)
+        w1_raw[0, 1] = load_weight("w1", w1, 0, P, P)
         inc_t = load("inc_t", inc, U16)
         sn_t = load("sn_t", sn, F32)
+        w1_raw[1, 1] = load_weight("w1", w1, 1, P, P)
         w2_raw = [load_weight("w2", w2, o) for o in range(PASSES)]
+        tail_t = load("tail_t", tail, U16)
+        w3_raw = [load_weight("w3", w3, o) for o in range(PASSES)]
+        head_t = load("head_t", head, U16)
         tri_t = load("tri_t", tri, U16)
         trj_t = load("trj_t", trj, U16)
         sa_t = load("sa_t", sa, F32)
         sb_t = load("sb_t", sb, F32)
         face_t = load("face_t", face, U16)
-        head_t = load("head_t", head, U16)
-        tail_t = load("tail_t", tail, U16)
         sf_t = load("sf_t", sf, F32)
-        w3_raw = [load_weight("w3", w3, o) for o in range(PASSES)]
 
-        x_pick = [sbuf("x_pick%d" % o, [P, S], U32) for o in range(PASSES)]
+        def cols(lst, e0, e1):
+            return lst[:, e0 // 16 : e1 // 16]
+
+        halves = [(0, HALF), (HALF, S)]
+        x_pick0 = sbuf("x_pick0", [P, S], U32)
+        x_pick1 = [sbuf("x_pick1%d" % i, [P, HALF], U32) for i in range(2)]
         scale_pick = sbuf("scale_pick", [P, S], U8)
-        nc.vector.tensor_copy(x_pick[0][:], x_all[0][:].indirect(offs_t[:]))
-        nc.vector.tensor_copy(x_pick[1][:], x_all[1][:].indirect(offs_t[:]))
         nc.vector.tensor_copy(scale_pick[:], scale_all[:].indirect(offs_t[:]))
+        nc.vector.tensor_copy(x_pick0[:], x_all[0][:].indirect(offs_t[:]))
 
-        def interleave(name, raw, c0, width, copy):
-            t = sbuf(name, [P, width, PACK], BF16)
-            copy(
-                t[:].rearrange("p (c i) t -> p c t i", i=4),
+        def interleave(dst, raw, c0, width):
+            nc.scalar.copy(
+                dst.rearrange("p (c i) t -> p c t i", i=4),
                 raw[:, :, c0 : c0 + width].rearrange("p t (c i) -> p c t i", i=4),
             )
-            return t
 
         def quantize(name, grouped, width):
             codes = sbuf(name + "_codes", [P, width], U32)
             scales = sbuf(name + "_scales", [P, width], U8)
             nc.vector.quantize_mx(
-                out=codes[:].bitcast(FP8X4), scales=scales[:], in_=grouped[:].rearrange("p c t -> p (c t)")
+                out=codes[:].bitcast(FP8X4), scales=scales[:], in_=grouped.rearrange("p c t -> p (c t)")
             )
             return codes, scales
 
-        def project(name, wq, c0, n0, n1):
-            acc = psum.tile([P, n1 - n0], F32, name=name)
+        def mx_pass(acc, wq, c0, o, e0, e1, start, stop):
+            codes, scales = wq
+            moving = x_pick0[:, e0:e1] if o == 0 else x_pick1[e0 // HALF][:]
+            nc.tensor.matmul_mx(
+                out=acc,
+                lhsT=codes[:, c0 : c0 + P].bitcast(FP8X4),
+                lhsT_scale=scales[:, c0 : c0 + P],
+                rhs=moving.bitcast(FP8X4),
+                rhs_scale=scale_pick[SCALE_ROWS * o :, e0:e1],
+                start=start,
+                stop=stop,
+            )
+
+        def project(acc, wq, b):
+            for e0, e1 in halves:
+                for o in range(PASSES):
+                    mx_pass(acc[:, e0:e1], wq, o * N + b * P, o, e0, e1, o == 0, o == PASSES - 1)
+
+        def y_block(b):
+            acc = [bank("y%d%d" % (b, i), 2 * b + i, HALF) for i in range(2)]
             for o in range(PASSES):
-                codes, scales = wq[o]
-                nc.tensor.matmul_mx(
-                    out=acc[:],
-                    lhsT=codes[:, c0 : c0 + P].bitcast(FP8X4),
-                    lhsT_scale=scales[:, c0 : c0 + P],
-                    rhs=x_pick[o][:, n0:n1].bitcast(FP8X4),
-                    rhs_scale=scale_pick[SCALE_ROWS * o :, n0:n1],
-                    start=(o == 0),
-                    stop=(o == PASSES - 1),
-                )
-            return acc
+                g = sbuf("g1_%d%d" % (o, b), [P, P, PACK], BF16)
+                interleave(g[:], w1_raw[o, b], 0, P)
+                wq = quantize("q1_%d%d" % (o, b), g[:], P)
+                if o == 1 and b == 0:
+                    for i, (e0, e1) in enumerate(halves):
+                        nc.vector.tensor_copy(x_pick1[i][:], x_all[1][:].indirect(cols(offs_t, e0, e1)))
+                for i, (e0, e1) in enumerate(halves):
+                    mx_pass(acc[i][:], wq, 0, o, e0, e1, o == 0, o == PASSES - 1)
+            copy = nc.vector.tensor_copy if b == 0 else nc.scalar.copy
+            for i, (e0, e1) in enumerate(halves):
+                copy(y_win[b][:, e0:e1], acc[i][:])
 
-        g00 = interleave("g1_00", w1_raw[0], 0, P, nc.scalar.copy)
-        q00 = quantize("q1_00", g00, P)
-        g01 = interleave("g1_01", w1_raw[0], P, P, nc.scalar.copy)
-        g10 = interleave("g1_10", w1_raw[1], 0, P, nc.vector.tensor_copy)
-        q01 = quantize("q1_01", g01, P)
-        q10 = quantize("q1_10", g10, P)
-        g11 = interleave("g1_11", w1_raw[1], P, P, nc.scalar.copy)
-        ya = project("y0a", [q00, q10], 0, 0, HALF)
-        yb = project("y0b", [q00, q10], 0, HALF, S)
-        q11 = quantize("q1_11", g11, P)
-        nc.vector.tensor_copy(y_win[0][:, 0:HALF], ya[:])
-        nc.scalar.copy(y_win[0][:, HALF:S], yb[:])
-        y1 = project("y1", [q01, q11], 0, 0, S)
-        nc.scalar.copy(y_win[1][:, 0:S], y1[:])
-
-        g2 = [interleave("g2_%d" % o, w2_raw[o], 0, N, nc.scalar.copy) for o in range(PASSES)]
-        li = [sbuf("li%d" % b, [P, S], F32) for b in range(BLOCKS)]
-        nc.vector.tensor_tensor(li[0][:], y_win[0][:].indirect(inc_t[:]), sn_t[:], MULT)
-        q2 = [quantize("q2_0", g2[0], N)]
-        nc.vector.tensor_tensor(li[1][:], y_win[1][:].indirect(inc_t[:]), sn_t[:], MULT)
-        q2.append(quantize("q2_1", g2[1], N))
-        for b in range(BLOCKS):
-            acc = project("h%d" % b, q2, b * P, 0, S)
-            nc.scalar.copy(h_win[b][:], acc[:])
-        for b in range(BLOCKS):
-            pairs = li[b][:].rearrange("p (v d) -> p d v", d=2)
+        def divergence(b):
+            li = sbuf("li%d" % b, [P, S], F32)
+            nc.vector.tensor_tensor(li[:], y_win[b][:].indirect(inc_t[:]), sn_t[:], MULT)
+            pairs = li[:].rearrange("p (v d) -> p d v", d=2)
             nc.vector.tensor_tensor(dv_win[b][:, 0:V], pairs[:, 0, :], pairs[:, 1, :], ADD)
 
-        g3 = [interleave("g3_%d" % o, w3_raw[o], 0, N, nc.scalar.copy) for o in range(PASSES)]
-        ca = [sbuf("ca%d" % b, [P, V], F32) for b in range(BLOCKS)]
-        cb = [sbuf("cb%d" % b, [P, V], F32) for b in range(BLOCKS)]
-        for b in range(BLOCKS):
-            nc.vector.tensor_tensor(ca[b][:], h_win[b][:].indirect(tri_t[:]), sa_t[:], MULT)
-            nc.vector.tensor_tensor(cb[b][:], h_win[b][:].indirect(trj_t[:]), sb_t[:], MULT)
-        q3 = []
-        for b in range(BLOCKS):
-            nc.vector.tensor_tensor(cu_win[b][:, 0:V], ca[b][:], cb[b][:], ADD)
-            q3.append(quantize("q3_%d" % b, g3[b], N))
-        own = [project("own%d" % b, q3, b * P, 0, S) for b in range(BLOCKS)]
+        def quantize_whole(name, raw):
+            g = sbuf("g" + name, [P, PASSES * N, PACK], BF16)
+            for o in range(PASSES):
+                interleave(g[:, o * N : (o + 1) * N, :], raw[o], 0, N)
+            return quantize("q" + name, g[:], PASSES * N)
 
-        def cols(lst, e0, e1):
-            return lst[:, e0 // 16 : e1 // 16]
+        def project_out(name, wq, b, i, dst):
+            acc = bank(name, i, S)
+            project(acc, wq, b)
+            nc.scalar.copy(dst, acc[:])
 
-        pieces = [(0, 0, S), (1, 0, HALF), (1, HALF, S)]
-        up, t1, t2 = {}, {}, {}
+        def curl(b, sides, up):
+            nc.vector.tensor_tensor(sides[:, 0:V], h_win[b][:].indirect(tri_t[:]), sa_t[:], MULT)
+            nc.vector.tensor_tensor(sides[:, V:], h_win[b][:].indirect(trj_t[:]), sb_t[:], MULT)
+            nc.vector.tensor_tensor(cu_win[b][:, 0:V], sides[:, 0:V], sides[:, V:], ADD)
+            nc.vector.tensor_tensor(up, cu_win[b][:].indirect(face_t[:]), sf_t[:], MULT)
 
-        def stage(i, k):
-            b, e0, e1 = pieces[i]
-            n = e1 - e0
-            if k == 0:
-                up[i] = sbuf("up%d" % i, [P, n], F32)
-                nc.vector.tensor_tensor(up[i][:], cu_win[b][:].indirect(cols(face_t, e0, e1)), sf_t[:, e0:e1], MULT)
-            elif k == 1:
-                t1[i] = sbuf("t1_%d" % i, [P, n], F32)
-                nc.vector.tensor_tensor(t1[i][:], dv_win[b][:].indirect(cols(head_t, e0, e1)), up[i][:], ADD)
-            elif k == 2:
-                t2[i] = sbuf("t2_%d" % i, [P, n], F32)
-                nc.vector.tensor_tensor(t2[i][:], dv_win[b][:].indirect(cols(tail_t, e0, e1)), t1[i][:], SUB)
-            else:
-                pre = sbuf("pre%d" % i, [P, n], F32)
-                nc.vector.tensor_tensor(pre[:], own[b][:, e0:e1], t2[i][:], SUB)
-                res = sbuf("res%d" % i, [P, n], F32)
-                nc.scalar.activation(res[:], pre[:], TANH)
-                nc.sync.dma_start(out[b * P : (b + 1) * P, e0:e1], res[:])
+        def add_term(b, term, first=False, last=False):
+            for i in range(2):
+                for c in range(2):
+                    e0 = i * HALF + c * P
+                    nc.tensor.matmul(
+                        sums[b, i][:, c * P : (c + 1) * P],
+                        term[:, e0 : e0 + P],
+                        ident[:],
+                        start=first and c == 0,
+                        stop=last and c == 1,
+                        is_transpose=True,
+                    )
 
-        for step in range(len(pieces) + 3):
-            for i in range(len(pieces)):
-                if 0 <= step - i < 4:
-                    stage(i, step - i)
+        def turn_back(b, i, func):
+            turned = sbuf("turned%d%d" % (b, i), [P, HALF], F32)
+            func(turned[:], sums[b, i][:])
+            back = bank("back%d%d" % (b, i), 4 + i, HALF)
+            for c in range(2):
+                nc.tensor.transpose(back[:, c * P : (c + 1) * P], turned[:, c * P : (c + 1) * P], ident[:])
+            return back
+
+        def leave(b, i, back):
+            t = sbuf("left%d%d" % (b, i), [P, HALF], F32)
+            nc.scalar.copy(t[:], back[:])
+            return t
+
+        y_block(0)
+        divergence(0)
+        y_block(1)
+        tail0 = sbuf("tail0", [P, S], F32, tag="g1_11")
+        nc.vector.tensor_copy(tail0[:], dv_win[0][:].indirect(tail_t[:]))
+        divergence(1)
+        q2 = quantize_whole("2", w2_raw)
+        down0 = sbuf("down0", [P, S], F32, tag="g2")
+        nc.vector.tensor_tensor(down0[:], dv_win[0][:].indirect(head_t[:]), tail0[:], SUB)
+        for b in (1, 0):
+            project_out("h%d" % b, q2, b, 4 + b, h_win[b][:])
+        q3 = quantize_whole("3", w3_raw)
+        own = [sbuf("own%d" % b, [P, S], F32) for b in range(BLOCKS)]
+        for b in (1, 0):
+            project_out("own%d" % b, q3, b, 6 + b, own[b][:])
+
+        sums = {(b, i): bank("sum%d%d" % (b, i), 2 * b + i, HALF) for b in range(BLOCKS) for i in range(2)}
+        late = sbuf("late", [P, 2 * S], F32, tag="g3")
+        sides1 = sbuf("sides1", [P, 2 * V], F32)
+        up0 = sbuf("up0", [P, S], F32)
+        up1 = late[:, 0:S]
+        curl(1, sides1[:], up1)
+        add_term(1, own[1][:], first=True)
+        add_term(1, up1, last=True)
+        backs = [turn_back(1, i, nc.scalar.copy) for i in range(2)]
+        rest = [leave(1, i, backs[i]) for i in range(2)]
+
+        add_term(0, own[0][:], first=True)
+        add_term(0, down0[:])
+        curl(0, late[:, S:], up0[:])
+        add_term(0, up0[:], last=True)
+        backs = [turn_back(0, i, lambda o, a: nc.scalar.activation(o, a, TANH)) for i in range(2)]
+        for i, (e0, e1) in enumerate(halves):
+            res = leave(0, i, backs[i])
+            nc.sync.dma_start(out[0:P, e0:e1], res[:])
+
+        part = [sbuf("part%d" % i, [P, HALF], F32) for i in range(2)]
+        for i, (e0, e1) in enumerate(halves):
+            nc.vector.tensor_tensor(part[i][:], dv_win[1][:].indirect(cols(head_t, e0, e1)), rest[i][:], ADD)
+        for i, (e0, e1) in enumerate(halves):
+            neg = sbuf("neg%d" % i, [P, HALF], F32)
+            nc.vector.tensor_tensor(neg[:], dv_win[1][:].indirect(cols(tail_t, e0, e1)), part[i][:], SUB)
+            res = sbuf("res%d" % i, [P, HALF], F32)
+            nc.scalar.activation(res[:], neg[:], TANH, scale=-1.0)
+            nc.sync.dma_start(out[P : 2 * P, e0:e1], res[:])

@@ -46,10 +46,11 @@ def tile_picked_yhodge_tanh_p_kernel(
             nc.sync.dma_start(t[:], src)
             return t
 
+
         def load_words(o):
             t = sbuf("x_all%d" % o, [P, T], U32)
             nc.sync.dma_start(t[:].bitcast(I32), x_words[o].rearrange("p c r -> p (c r)").bitcast(I32))
-            return t
+            return t[:]
 
         def load_weight(name, w, o, c0=0, width=N):
             t = sbuf("%s_raw%d_%d" % (name, o, c0), [P, PACK, width], F32)
@@ -61,7 +62,7 @@ def tile_picked_yhodge_tanh_p_kernel(
         nc.gpsimd.memset(scale_all[:].bitcast(I32), 0)
         zeros = sbuf("zeros", [P, SPARE], F32)
         nc.vector.memset(zeros[:], 0.0)
-        y_win = [sbuf("y_win%d" % b, [P, S + SPARE], F32) for b in range(BLOCKS)]
+        y_win = [sbuf("y_win0", [P, S + SPARE], F32)]
         h_win = [sbuf("h_win%d" % b, [P, S], F32) for b in range(BLOCKS)]
         dv_win = [sbuf("dv_win%d" % b, [P, 2 * S], F32) for b in range(BLOCKS)]
         ident = sbuf("ident", [P, P], F32)
@@ -71,22 +72,21 @@ def tile_picked_yhodge_tanh_p_kernel(
         offs_t = load("offs_t", offs, U16)
         x_all = [load_words(0)]
         for q in range(4):
-            nc.scalar.dma_start(
+            nc.sync.dma_start(
                 scale_all[32 * q : 32 * q + PASSES * SCALE_ROWS, :].bitcast(I32),
                 x_scales[:, SCALE_ROWS * q : SCALE_ROWS * (q + 1), :].bitcast(I32),
             )
+        nc.scalar.activation(y_win[0][:, S:], zeros[:], TANH)
         for b in range(BLOCKS):
-            nc.scalar.activation(y_win[b][:, S:], zeros[:], TANH)
             nc.vector.memset(dv_win[b][:, V:], 0.0)
             nc.vector.memset(cu_win[b][:, V:], 0.0)
-        w1_raw = {(0, 0): load_weight("w1", w1, 0, 0, P)}
+        w1_raw = [load_weight("w1", w1, 0)]
         x_all.append(load_words(1))
-        w1_raw[1, 0] = load_weight("w1", w1, 1, 0, P)
-        w1_raw[0, 1] = load_weight("w1", w1, 0, P, P)
+        w1_raw.append(load_weight("w1", w1, 1))
         inc_t = load("inc_t", inc, U16)
+        w2_raw = [load_weight("w2", w2, 0)]
         sn_t = load("sn_t", sn, F32)
-        w1_raw[1, 1] = load_weight("w1", w1, 1, P, P)
-        w2_raw = [load_weight("w2", w2, o) for o in range(PASSES)]
+        w2_raw.append(load_weight("w2", w2, 1))
         tail_t = load("tail_t", tail, U16)
         w3_raw = [load_weight("w3", w3, o) for o in range(PASSES)]
         head_t = load("head_t", head, U16)
@@ -101,14 +101,13 @@ def tile_picked_yhodge_tanh_p_kernel(
             return lst[:, e0 // 16 : e1 // 16]
 
         halves = [(0, HALF), (HALF, S)]
-        x_pick0 = sbuf("x_pick0", [P, S], U32)
-        x_pick1 = [sbuf("x_pick1%d" % i, [P, HALF], U32) for i in range(2)]
+        x_pick = [sbuf("x_pick%d" % o, [P, S], U32) for o in range(PASSES)]
         scale_pick = sbuf("scale_pick", [P, S], U8)
         nc.vector.tensor_copy(scale_pick[:], scale_all[:].indirect(offs_t[:]))
-        nc.vector.tensor_copy(x_pick0[:], x_all[0][:].indirect(offs_t[:]))
+        nc.vector.tensor_copy(x_pick[0][:], x_all[0].indirect(offs_t[:]))
 
-        def interleave(dst, raw, c0, width):
-            nc.scalar.copy(
+        def interleave(dst, raw, c0, width, copy=nc.scalar.copy):
+            copy(
                 dst.rearrange("p (c i) t -> p c t i", i=4),
                 raw[:, :, c0 : c0 + width].rearrange("p t (c i) -> p c t i", i=4),
             )
@@ -123,66 +122,54 @@ def tile_picked_yhodge_tanh_p_kernel(
 
         def mx_pass(acc, wq, c0, o, e0, e1, start, stop):
             codes, scales = wq
-            moving = x_pick0[:, e0:e1] if o == 0 else x_pick1[e0 // HALF][:]
             nc.tensor.matmul_mx(
                 out=acc,
                 lhsT=codes[:, c0 : c0 + P].bitcast(FP8X4),
                 lhsT_scale=scales[:, c0 : c0 + P],
-                rhs=moving.bitcast(FP8X4),
+                rhs=x_pick[o][:, e0:e1].bitcast(FP8X4),
                 rhs_scale=scale_pick[SCALE_ROWS * o :, e0:e1],
                 start=start,
                 stop=stop,
             )
 
-        def project(acc, wq, b):
-            for e0, e1 in halves:
-                for o in range(PASSES):
-                    mx_pass(acc[:, e0:e1], wq, o * N + b * P, o, e0, e1, o == 0, o == PASSES - 1)
-
         def y_block(b):
             acc = [bank("y%d%d" % (b, i), 2 * b + i, HALF) for i in range(2)]
             for o in range(PASSES):
                 g = sbuf("g1_%d%d" % (o, b), [P, P, PACK], BF16)
-                interleave(g[:], w1_raw[o, b], 0, P)
+                interleave(g[:], w1_raw[o], b * P, P)
                 wq = quantize("q1_%d%d" % (o, b), g[:], P)
                 if o == 1 and b == 0:
                     for i, (e0, e1) in enumerate(halves):
-                        nc.vector.tensor_copy(x_pick1[i][:], x_all[1][:].indirect(cols(offs_t, e0, e1)))
+                        nc.vector.tensor_copy(x_pick[1][:, e0:e1], x_all[1].indirect(cols(offs_t, e0, e1)))
                 for i, (e0, e1) in enumerate(halves):
                     mx_pass(acc[i][:], wq, 0, o, e0, e1, o == 0, o == PASSES - 1)
-            copy = nc.vector.tensor_copy if b == 0 else nc.scalar.copy
-            for i, (e0, e1) in enumerate(halves):
-                copy(y_win[b][:, e0:e1], acc[i][:])
+            return acc
 
         def divergence(b):
-            li = sbuf("li%d" % b, [P, S], F32)
+            li = sbuf("li%d" % b, [P, S], F32, tag="g1_11" if b == 0 else None)
             nc.vector.tensor_tensor(li[:], y_win[b][:].indirect(inc_t[:]), sn_t[:], MULT)
             pairs = li[:].rearrange("p (v d) -> p d v", d=2)
             nc.vector.tensor_tensor(dv_win[b][:, 0:V], pairs[:, 0, :], pairs[:, 1, :], ADD)
 
-        def quantize_whole(name, raw):
-            g = sbuf("g" + name, [P, PASSES * N, PACK], BF16)
+        def group(name, raw):
+            g = sbuf(name, [P, N, PACK], BF16)
+            interleave(g[:], raw, 0, N)
+            return g
+
+        def project(name, first_bank, grouped):
+            acc = [bank("%s%d" % (name, b), first_bank + b, S) for b in range(BLOCKS)]
             for o in range(PASSES):
-                interleave(g[:, o * N : (o + 1) * N, :], raw[o], 0, N)
-            return quantize("q" + name, g[:], PASSES * N)
+                wq = quantize("q%s_%d" % (name, o), grouped(o)[:], N)
+                for b in range(BLOCKS):
+                    mx_pass(acc[b][:], wq, b * P, o, 0, S, o == 0, o == PASSES - 1)
+            return acc
 
-        def project_out(name, wq, b, i, dst):
-            acc = bank(name, i, S)
-            project(acc, wq, b)
-            nc.scalar.copy(dst, acc[:])
-
-        def curl(b, sides, up):
-            nc.vector.tensor_tensor(sides[:, 0:V], h_win[b][:].indirect(tri_t[:]), sa_t[:], MULT)
-            nc.vector.tensor_tensor(sides[:, V:], h_win[b][:].indirect(trj_t[:]), sb_t[:], MULT)
-            nc.vector.tensor_tensor(cu_win[b][:, 0:V], sides[:, 0:V], sides[:, V:], ADD)
-            nc.vector.tensor_tensor(up, cu_win[b][:].indirect(face_t[:]), sf_t[:], MULT)
-
-        def add_term(b, term, first=False, last=False):
+        def add_term(term, first=False, last=False):
             for i in range(2):
                 for c in range(2):
                     e0 = i * HALF + c * P
                     nc.tensor.matmul(
-                        sums[b, i][:, c * P : (c + 1) * P],
+                        sums[i][:, c * P : (c + 1) * P],
                         term[:, e0 : e0 + P],
                         ident[:],
                         start=first and c == 0,
@@ -190,61 +177,68 @@ def tile_picked_yhodge_tanh_p_kernel(
                         is_transpose=True,
                     )
 
-        def turn_back(b, i, func):
-            turned = sbuf("turned%d%d" % (b, i), [P, HALF], F32)
-            func(turned[:], sums[b, i][:])
-            back = bank("back%d%d" % (b, i), 4 + i, HALF)
+        y_acc = y_block(0)
+        for i, (e0, e1) in enumerate(halves):
+            nc.vector.tensor_copy(y_win[0][:, e0:e1], y_acc[i][:])
+        y_acc = y_block(1)
+        gh_first = group("gh_0", w2_raw[0])
+        y_win.append(sbuf("y_win1", [P, S + SPARE], F32, tag="w2_raw0_0"))
+        nc.scalar.copy(y_win[1][:, S:], zeros[:])
+        for i, (e0, e1) in enumerate(halves):
+            nc.scalar.copy(y_win[1][:, e0:e1], y_acc[i][:])
+        divergence(0)
+        divergence(1)
+        h_acc = project("h", 4, lambda o: gh_first if o == 0 else group("gh_1", w2_raw[1]))
+        for b in range(BLOCKS):
+            nc.scalar.copy(h_win[b][:], h_acc[b][:])
+        ends0 = sbuf("ends0", [P, 2 * S], F32, tag="gh_1")
+        tail0 = ends0[:, 0:S]
+        down0 = ends0[:, S:]
+        nc.vector.tensor_copy(tail0, dv_win[0][:].indirect(tail_t[:]))
+        nc.vector.tensor_tensor(down0, dv_win[0][:].indirect(head_t[:]), tail0, SUB)
+        own = project("own", 6, lambda o: group("gown_%d" % o, w3_raw[o]))
+        own0 = sbuf("own0", [P, S], F32)
+        nc.scalar.copy(own0[:], own[0][:])
+
+        for b in range(BLOCKS):
+            sides = sbuf("sides%d" % b, [P, 2 * V], F32)
+            nc.vector.tensor_tensor(sides[:, 0:V], h_win[b][:].indirect(tri_t[:]), sa_t[:], MULT)
+            nc.vector.tensor_tensor(sides[:, V:], h_win[b][:].indirect(trj_t[:]), sb_t[:], MULT)
+            nc.vector.tensor_tensor(cu_win[b][:, 0:V], sides[:, 0:V], sides[:, V:], ADD)
+
+        up0 = sbuf("up0", [P, S], F32)
+        nc.vector.tensor_tensor(up0[:], cu_win[0][:].indirect(face_t[:]), sf_t[:], MULT)
+        sums = [bank("sum%d" % i, i, HALF) for i in range(2)]
+        add_term(own0[:], first=True)
+        add_term(down0)
+        add_term(up0[:], last=True)
+        backs = []
+        for i in range(2):
+            turned = sbuf("turned%d" % i, [P, HALF], F32)
+            nc.scalar.activation(turned[:], sums[i][:], TANH)
+            back = bank("back%d" % i, 2 + i, HALF)
             for c in range(2):
                 nc.tensor.transpose(back[:, c * P : (c + 1) * P], turned[:, c * P : (c + 1) * P], ident[:])
-            return back
-
-        def leave(b, i, back):
-            t = sbuf("left%d%d" % (b, i), [P, HALF], F32)
-            nc.scalar.copy(t[:], back[:])
-            return t
-
-        y_block(0)
-        divergence(0)
-        y_block(1)
-        tail0 = sbuf("tail0", [P, S], F32, tag="g1_11")
-        nc.vector.tensor_copy(tail0[:], dv_win[0][:].indirect(tail_t[:]))
-        divergence(1)
-        q2 = quantize_whole("2", w2_raw)
-        down0 = sbuf("down0", [P, S], F32, tag="g2")
-        nc.vector.tensor_tensor(down0[:], dv_win[0][:].indirect(head_t[:]), tail0[:], SUB)
-        for b in (1, 0):
-            project_out("h%d" % b, q2, b, 4 + b, h_win[b][:])
-        q3 = quantize_whole("3", w3_raw)
-        own = [sbuf("own%d" % b, [P, S], F32) for b in range(BLOCKS)]
-        for b in (1, 0):
-            project_out("own%d" % b, q3, b, 6 + b, own[b][:])
-
-        sums = {(b, i): bank("sum%d%d" % (b, i), 2 * b + i, HALF) for b in range(BLOCKS) for i in range(2)}
-        late = sbuf("late", [P, 2 * S], F32, tag="g3")
-        sides1 = sbuf("sides1", [P, 2 * V], F32)
-        up0 = sbuf("up0", [P, S], F32)
-        up1 = late[:, 0:S]
-        curl(1, sides1[:], up1)
-        add_term(1, own[1][:], first=True)
-        add_term(1, up1, last=True)
-        backs = [turn_back(1, i, nc.scalar.copy) for i in range(2)]
-        rest = [leave(1, i, backs[i]) for i in range(2)]
-
-        add_term(0, own[0][:], first=True)
-        add_term(0, down0[:])
-        curl(0, late[:, S:], up0[:])
-        add_term(0, up0[:], last=True)
-        backs = [turn_back(0, i, lambda o, a: nc.scalar.activation(o, a, TANH)) for i in range(2)]
+            backs.append(back)
         for i, (e0, e1) in enumerate(halves):
-            res = leave(0, i, backs[i])
+            res = sbuf("res0%d" % i, [P, HALF], F32)
+            nc.scalar.copy(res[:], backs[i][:])
             nc.sync.dma_start(out[0:P, e0:e1], res[:])
 
-        part = [sbuf("part%d" % i, [P, HALF], F32) for i in range(2)]
-        for i, (e0, e1) in enumerate(halves):
-            nc.vector.tensor_tensor(part[i][:], dv_win[1][:].indirect(cols(head_t, e0, e1)), rest[i][:], ADD)
-        for i, (e0, e1) in enumerate(halves):
-            neg = sbuf("neg%d" % i, [P, HALF], F32)
-            nc.vector.tensor_tensor(neg[:], dv_win[1][:].indirect(cols(tail_t, e0, e1)), part[i][:], SUB)
-            res = sbuf("res%d" % i, [P, HALF], F32)
-            nc.scalar.activation(res[:], neg[:], TANH, scale=-1.0)
+        def step(name, e0, e1, first, second, op):
+            t = sbuf("%s%d" % (name, e0), [P, e1 - e0], F32)
+            nc.vector.tensor_tensor(t[:], first, second, op)
+            return t
+
+        run = {}
+        for e0, e1 in halves:
+            run[e0] = step("up1", e0, e1, cu_win[1][:].indirect(cols(face_t, e0, e1)), sf_t[:, e0:e1], MULT)
+        for e0, e1 in halves:
+            run[e0] = step("plus", e0, e1, dv_win[1][:].indirect(cols(head_t, e0, e1)), run[e0][:], ADD)
+        for e0, e1 in halves:
+            run[e0] = step("neg", e0, e1, dv_win[1][:].indirect(cols(tail_t, e0, e1)), run[e0][:], SUB)
+        for e0, e1 in halves:
+            pre = step("pre", e0, e1, own[1][:, e0:e1], run[e0][:], SUB)
+            res = sbuf("res1%d" % e0, [P, HALF], F32)
+            nc.scalar.activation(res[:], pre[:], TANH)
             nc.sync.dma_start(out[P : 2 * P, e0:e1], res[:])

@@ -33,6 +33,7 @@ def tile_picked_yhodge_tanh_p_kernel(
     nc = tc.nc
     with ExitStack() as ctx:
         keep = ctx.enter_context(tc.tile_pool(name="keep", bufs=1))
+        shared = ctx.enter_context(tc.tile_pool(name="shared", bufs=1))
         psum = ctx.enter_context(tc.psum_pool(name="psum", bufs=1))
 
         def sbuf(name, shape, dtype, tag=None):
@@ -52,8 +53,9 @@ def tile_picked_yhodge_tanh_p_kernel(
             nc.sync.dma_start(t[:].bitcast(I32), x_words[o].rearrange("p c r -> p (c r)").bitcast(I32))
             return t[:]
 
-        def load_weight(name, w, o, c0=0, width=N):
-            t = sbuf("%s_raw%d_%d" % (name, o, c0), [P, PACK, width], F32)
+        def load_weight(name, w, o, c0=0, width=N, t=None):
+            if t is None:
+                t = sbuf("%s_raw%d" % (name, o), [P, PACK, width], F32)
             rows = w[o * K_PASS : (o + 1) * K_PASS, c0 : c0 + width]
             nc.sync.dma_start(t[:], rows.rearrange("(p t) c -> p t c", t=PACK))
             return t
@@ -63,11 +65,17 @@ def tile_picked_yhodge_tanh_p_kernel(
         zeros = sbuf("zeros", [P, SPARE], F32)
         nc.vector.memset(zeros[:], 0.0)
         y_win = [sbuf("y_win0", [P, S + SPARE], F32)]
-        h_win = [sbuf("h_win%d" % b, [P, S], F32) for b in range(BLOCKS)]
-        dv_win = [sbuf("dv_win%d" % b, [P, 2 * S], F32) for b in range(BLOCKS)]
+        h_win = []
+        dv_win = [sbuf("dv_win0", [P, S], F32), sbuf("dv_win1", [P, V + S], F32)]
+        cu_win = [sbuf("cu_win0", [P, S + SPARE], F32), sbuf("cu_win1", [P, V + SPARE], F32)]
+        nc.vector.memset(cu_win[0][:, S:], 0.0)
+        nc.vector.memset(cu_win[1][:, V:], 0.0)
         ident = sbuf("ident", [P, P], F32)
         make_identity(nc, ident[:])
-        cu_win = [sbuf("cu_win%d" % b, [P, S + SPARE], F32) for b in range(BLOCKS)]
+        sn_t = dv_win[0]
+        sf_t = dv_win[1][:, V:]
+        sa_t = cu_win[0][:, 0:V]
+        sb_t = cu_win[0][:, V:S]
 
         offs_t = load("offs_t", offs, U16)
         x_all = [load_words(0)]
@@ -77,25 +85,24 @@ def tile_picked_yhodge_tanh_p_kernel(
                 x_scales[:, SCALE_ROWS * q : SCALE_ROWS * (q + 1), :].bitcast(I32),
             )
         nc.scalar.activation(y_win[0][:, S:], zeros[:], TANH)
-        for b in range(BLOCKS):
-            nc.vector.memset(dv_win[b][:, V:], 0.0)
-            nc.vector.memset(cu_win[b][:, V:], 0.0)
-        w1_raw = [load_weight("w1", w1, 0)]
+        w1_first = load_weight("w1", w1, 0)
+        w1_raw = {(0, 0): w1_first[:, :, 0:P], (0, 1): w1_first[:, :, P:N]}
+        w1_raw[1, 0] = load_weight("w1a", w1, 1, 0, P)[:]
         x_all.append(load_words(1))
-        w1_raw.append(load_weight("w1", w1, 1))
+        w1_raw[1, 1] = load_weight("w1b", w1, 1, P, P)[:]
         inc_t = load("inc_t", inc, U16)
-        w2_raw = [load_weight("w2", w2, 0)]
-        sn_t = load("sn_t", sn, F32)
-        w2_raw.append(load_weight("w2", w2, 1))
+        nc.sync.dma_start(sn_t[:], sn)
+        w2_raw = [load_weight("w2", w2, o) for o in range(PASSES)]
         tail_t = load("tail_t", tail, U16)
-        w3_raw = [load_weight("w3", w3, o) for o in range(PASSES)]
         head_t = load("head_t", head, U16)
         tri_t = load("tri_t", tri, U16)
         trj_t = load("trj_t", trj, U16)
-        sa_t = load("sa_t", sa, F32)
-        sb_t = load("sb_t", sb, F32)
+        nc.sync.dma_start(sa_t, sa)
+        nc.sync.dma_start(sb_t, sb)
+        w3_last = shared.tile([P, PACK, N], F32, name="w3_last", offset=0)
+        w3_raw = [load_weight("w3", w3, 0), load_weight("w3", w3, 1, t=w3_last)]
         face_t = load("face_t", face, U16)
-        sf_t = load("sf_t", sf, F32)
+        nc.sync.dma_start(sf_t, sf)
 
         def cols(lst, e0, e1):
             return lst[:, e0 // 16 : e1 // 16]
@@ -103,8 +110,11 @@ def tile_picked_yhodge_tanh_p_kernel(
         halves = [(0, HALF), (HALF, S)]
         x_pick = [sbuf("x_pick%d" % o, [P, S], U32) for o in range(PASSES)]
         scale_pick = sbuf("scale_pick", [P, S], U8)
-        nc.vector.tensor_copy(scale_pick[:], scale_all[:].indirect(offs_t[:]))
         nc.vector.tensor_copy(x_pick[0][:], x_all[0].indirect(offs_t[:]))
+        nc.vector.tensor_copy(scale_pick[:], scale_all[:].indirect(offs_t[:]))
+
+        def grouped_view(words):
+            return words.bitcast(BF16).rearrange("p (c t) -> p c t", t=PACK)
 
         def interleave(dst, raw, c0, width, copy=nc.scalar.copy):
             copy(
@@ -113,14 +123,14 @@ def tile_picked_yhodge_tanh_p_kernel(
             )
 
         def quantize(name, grouped, width):
-            codes = sbuf(name + "_codes", [P, width], U32)
+            codes = sbuf(name + "_codes", [P, width], U32, tag=name + "_codes")
             scales = sbuf(name + "_scales", [P, width], U8)
             nc.vector.quantize_mx(
                 out=codes[:].bitcast(FP8X4), scales=scales[:], in_=grouped.rearrange("p c t -> p (c t)")
             )
             return codes, scales
 
-        def mx_pass(acc, wq, c0, o, e0, e1, start, stop):
+        def mx_pass(acc, wq, c0, o, e0, e1):
             codes, scales = wq
             nc.tensor.matmul_mx(
                 out=acc,
@@ -128,41 +138,93 @@ def tile_picked_yhodge_tanh_p_kernel(
                 lhsT_scale=scales[:, c0 : c0 + P],
                 rhs=x_pick[o][:, e0:e1].bitcast(FP8X4),
                 rhs_scale=scale_pick[SCALE_ROWS * o :, e0:e1],
-                start=start,
-                stop=stop,
+                start=o == 0,
+                stop=o == PASSES - 1,
             )
 
-        def y_block(b):
-            acc = [bank("y%d%d" % (b, i), 2 * b + i, HALF) for i in range(2)]
-            for o in range(PASSES):
-                g = sbuf("g1_%d%d" % (o, b), [P, P, PACK], BF16)
-                interleave(g[:], w1_raw[o], b * P, P)
-                wq = quantize("q1_%d%d" % (o, b), g[:], P)
-                if o == 1 and b == 0:
-                    for i, (e0, e1) in enumerate(halves):
-                        nc.vector.tensor_copy(x_pick[1][:, e0:e1], x_all[1].indirect(cols(offs_t, e0, e1)))
-                for i, (e0, e1) in enumerate(halves):
-                    mx_pass(acc[i][:], wq, 0, o, e0, e1, o == 0, o == PASSES - 1)
-            return acc
+        def fused(dst, window, lst, e0, e1, other, op):
+            nc.vector.tensor_tensor(dst, window[:].indirect(cols(lst, e0, e1)), other, op)
 
-        def divergence(b):
-            li = sbuf("li%d" % b, [P, S], F32, tag="g1_11" if b == 0 else None)
-            nc.vector.tensor_tensor(li[:], y_win[b][:].indirect(inc_t[:]), sn_t[:], MULT)
-            pairs = li[:].rearrange("p (v d) -> p d v", d=2)
+        pieces = [(0, HALF), (HALF, HALF + P), (HALF + P, S)]
+        y0_acc = [bank("y0%d" % i, (0, 1, 7)[i], e1 - e0) for i, (e0, e1) in enumerate(pieces)]
+        y1_acc = bank("y1", 2, S)
+        g1 = {}
+        for o, b in ((0, 0), (1, 0), (0, 1), (1, 1)):
+            g1[o, b] = sbuf("g1_%d%d" % (o, b), [P, P, PACK], BF16)
+            interleave(g1[o, b][:], w1_raw[o, b], 0, P)
+        wq = quantize("q1_00", g1[0, 0][:], P)
+        for i, (e0, e1) in enumerate(pieces):
+            mx_pass(y0_acc[i][:], wq, 0, 0, e0, e1)
+        wq = quantize("q1_10", g1[1, 0][:], P)
+        for i, (e0, e1) in enumerate(pieces):
+            nc.vector.tensor_copy(x_pick[1][:, e0:e1], x_all[1].indirect(cols(offs_t, e0, e1)))
+            mx_pass(y0_acc[i][:], wq, 0, 1, e0, e1)
+        for o in range(PASSES):
+            wq = quantize("q1_%d1" % o, g1[o, 1][:], P)
+            mx_pass(y1_acc[:], wq, 0, o, 0, S)
+        for i, (e0, e1) in enumerate(pieces):
+            copy = nc.scalar.copy if i == 0 else nc.vector.tensor_copy
+            copy(y_win[0][:, e0:e1], y0_acc[i][:])
+
+        li0 = sbuf("li0", [P, S], F32, tag="g1_11")
+        li1 = sbuf("li1", [P, S], F32)
+        g2_first = sbuf("g2_first", [P, N, PACK], BF16, tag="q1_11_codes")
+        li = [li0[:], li1[:]]
+        tail0 = sbuf("tail0", [P, S], F32)
+
+        def quantize_blocks(name, grouped, acc, o):
+            for b in range(BLOCKS):
+                wq = quantize("q%s%d%d" % (name, o, b), grouped[:, b * P : (b + 1) * P, :], P)
+                mx_pass(acc[b][:], wq, 0, o, 0, S)
+
+        fused(li[0], y_win[0], inc_t, 0, S, sn_t[:], MULT)
+        h_acc = [bank("h%d" % b, 3 + b, S) for b in range(BLOCKS)]
+        g2 = [g2_first[:], grouped_view(tail0[:])]
+        y_win.append(sbuf("y_win1", [P, S], F32))
+        nc.scalar.copy(y_win[1][:], y1_acc[:])
+        for o in range(PASSES):
+            interleave(g2[o], w2_raw[o], 0, N)
+        for e0, e1 in halves:
+            fused(li[1][:, e0:e1], y_win[1], inc_t, e0, e1, sn_t[:, e0:e1], MULT)
+        wq = quantize("qh0", g2[0], N)
+        for b in range(BLOCKS):
+            mx_pass(h_acc[b][:], wq, b * P, 0, 0, S)
+        for b in range(BLOCKS):
+            pairs = li[b].rearrange("p (v d) -> p d v", d=2)
             nc.vector.tensor_tensor(dv_win[b][:, 0:V], pairs[:, 0, :], pairs[:, 1, :], ADD)
+        quantize_blocks("h", g2[1], h_acc, 1)
+        g3 = [sbuf("g3_%d" % o, [P, N, PACK], BF16) for o in range(PASSES)]
+        for o in range(PASSES):
+            interleave(g3[o][:], w3_raw[o], 0, N)
+        for b in range(BLOCKS):
+            h_win.append(shared.tile([P, S], F32, name="h_win%d" % b, offset=b * S * 4))
+        for b in range(BLOCKS):
+            nc.scalar.copy(h_win[b][:], h_acc[b][:])
+        for e0, e1 in halves:
+            nc.vector.tensor_copy(tail0[:, e0:e1], dv_win[0][:].indirect(cols(tail_t, e0, e1)))
+        down0 = sbuf("down0", [P, S], F32)
+        fused(down0[:, 0:HALF], dv_win[0], head_t, 0, HALF, tail0[:, 0:HALF], SUB)
+        fused(down0[:, HALF:S], dv_win[0], head_t, HALF, S, tail0[:, HALF:S], SUB)
 
-        def group(name, raw):
-            g = sbuf(name, [P, N, PACK], BF16)
-            interleave(g[:], raw, 0, N)
-            return g
+        sides = [sbuf("sides0", [P, 2 * V], F32), sbuf("sides1", [P, 2 * V], F32)]
+        own = [bank("own%d" % b, 5 + b, S) for b in range(BLOCKS)]
+        for o in range(PASSES):
+            wq = quantize("qown%d" % o, g3[o][:], N)
+            for b in range(BLOCKS):
+                mx_pass(own[b][:], wq, b * P, o, 0, S)
+        fused(sides[0][:, 0:V], h_win[0], tri_t, 0, V, sa_t, MULT)
+        fused(sides[0][:, V:], h_win[0], trj_t, 0, V, sb_t, MULT)
+        fused(sides[1][:, 0:V], h_win[1], tri_t, 0, V, sa_t, MULT)
+        fused(sides[1][:, V:], h_win[1], trj_t, 0, V, sb_t, MULT)
+        own0 = sbuf("own0", [P, S], F32)
+        nc.scalar.copy(own0[:], own[0][:])
+        for b in range(BLOCKS):
+            nc.vector.tensor_tensor(cu_win[b][:, 0:V], sides[b][:, 0:V], sides[b][:, V:], ADD)
 
-        def project(name, first_bank, grouped):
-            acc = [bank("%s%d" % (name, b), first_bank + b, S) for b in range(BLOCKS)]
-            for o in range(PASSES):
-                wq = quantize("q%s_%d" % (name, o), grouped(o)[:], N)
-                for b in range(BLOCKS):
-                    mx_pass(acc[b][:], wq, b * P, o, 0, S, o == 0, o == PASSES - 1)
-            return acc
+        up0 = sbuf("up0", [P, S], F32)
+        fused(up0[:], cu_win[0], face_t, 0, S, sf_t, MULT)
+
+        sums = [bank("sum%d" % i, i, HALF) for i in range(2)]
 
         def add_term(term, first=False, last=False):
             for i in range(2):
@@ -177,40 +239,8 @@ def tile_picked_yhodge_tanh_p_kernel(
                         is_transpose=True,
                     )
 
-        y_acc = y_block(0)
-        for i, (e0, e1) in enumerate(halves):
-            nc.vector.tensor_copy(y_win[0][:, e0:e1], y_acc[i][:])
-        y_acc = y_block(1)
-        gh_first = group("gh_0", w2_raw[0])
-        y_win.append(sbuf("y_win1", [P, S + SPARE], F32, tag="w2_raw0_0"))
-        nc.scalar.copy(y_win[1][:, S:], zeros[:])
-        for i, (e0, e1) in enumerate(halves):
-            nc.scalar.copy(y_win[1][:, e0:e1], y_acc[i][:])
-        divergence(0)
-        divergence(1)
-        h_acc = project("h", 4, lambda o: gh_first if o == 0 else group("gh_1", w2_raw[1]))
-        for b in range(BLOCKS):
-            nc.scalar.copy(h_win[b][:], h_acc[b][:])
-        ends0 = sbuf("ends0", [P, 2 * S], F32, tag="gh_1")
-        tail0 = ends0[:, 0:S]
-        down0 = ends0[:, S:]
-        nc.vector.tensor_copy(tail0, dv_win[0][:].indirect(tail_t[:]))
-        nc.vector.tensor_tensor(down0, dv_win[0][:].indirect(head_t[:]), tail0, SUB)
-        own = project("own", 6, lambda o: group("gown_%d" % o, w3_raw[o]))
-        own0 = sbuf("own0", [P, S], F32)
-        nc.scalar.copy(own0[:], own[0][:])
-
-        for b in range(BLOCKS):
-            sides = sbuf("sides%d" % b, [P, 2 * V], F32)
-            nc.vector.tensor_tensor(sides[:, 0:V], h_win[b][:].indirect(tri_t[:]), sa_t[:], MULT)
-            nc.vector.tensor_tensor(sides[:, V:], h_win[b][:].indirect(trj_t[:]), sb_t[:], MULT)
-            nc.vector.tensor_tensor(cu_win[b][:, 0:V], sides[:, 0:V], sides[:, V:], ADD)
-
-        up0 = sbuf("up0", [P, S], F32)
-        nc.vector.tensor_tensor(up0[:], cu_win[0][:].indirect(face_t[:]), sf_t[:], MULT)
-        sums = [bank("sum%d" % i, i, HALF) for i in range(2)]
-        add_term(own0[:], first=True)
-        add_term(down0)
+        add_term(down0[:], first=True)
+        add_term(own0[:])
         add_term(up0[:], last=True)
         backs = []
         for i in range(2):
@@ -225,20 +255,18 @@ def tile_picked_yhodge_tanh_p_kernel(
             nc.scalar.copy(res[:], backs[i][:])
             nc.sync.dma_start(out[0:P, e0:e1], res[:])
 
-        def step(name, e0, e1, first, second, op):
-            t = sbuf("%s%d" % (name, e0), [P, e1 - e0], F32)
-            nc.vector.tensor_tensor(t[:], first, second, op)
-            return t
-
-        run = {}
+        up1 = sbuf("up1", [P, S], F32)
+        rest1 = sbuf("rest1", [P, S], F32)
+        plus1 = sbuf("plus1", [P, S], F32)
         for e0, e1 in halves:
-            run[e0] = step("up1", e0, e1, cu_win[1][:].indirect(cols(face_t, e0, e1)), sf_t[:, e0:e1], MULT)
+            fused(up1[:, e0:e1], cu_win[1], face_t, e0, e1, sf_t[:, e0:e1], MULT)
         for e0, e1 in halves:
-            run[e0] = step("plus", e0, e1, dv_win[1][:].indirect(cols(head_t, e0, e1)), run[e0][:], ADD)
+            nc.vector.tensor_tensor(rest1[:, e0:e1], own[1][:, e0:e1], up1[:, e0:e1], ADD)
         for e0, e1 in halves:
-            run[e0] = step("neg", e0, e1, dv_win[1][:].indirect(cols(tail_t, e0, e1)), run[e0][:], SUB)
-        for e0, e1 in halves:
-            pre = step("pre", e0, e1, own[1][:, e0:e1], run[e0][:], SUB)
-            res = sbuf("res1%d" % e0, [P, HALF], F32)
-            nc.scalar.activation(res[:], pre[:], TANH)
+            fused(plus1[:, e0:e1], dv_win[1], head_t, e0, e1, rest1[:, e0:e1], ADD)
+        for e0, e1 in ((0, HALF), (HALF, HALF + P), (HALF + P, S)):
+            neg = sbuf("neg%d" % e0, [P, e1 - e0], F32)
+            fused(neg[:], dv_win[1], tail_t, e0, e1, plus1[:, e0:e1], SUB)
+            res = sbuf("res1%d" % e0, [P, e1 - e0], F32)
+            nc.scalar.activation(res[:], neg[:], TANH, scale=-1.0)
             nc.sync.dma_start(out[P : 2 * P, e0:e1], res[:])

@@ -64,11 +64,10 @@ def tile_picked_yhodge_tanh_p_kernel(
         nc.gpsimd.memset(scale_all[:].bitcast(I32), 0)
         zeros = sbuf("zeros", [P, SPARE], F32)
         nc.vector.memset(zeros[:], 0.0)
-        y_win = [sbuf("y_win0", [P, S + SPARE], F32)]
+        y_win = []
         h_win = []
         dv_win = [sbuf("dv_win0", [P, S], F32), sbuf("dv_win1", [P, V + S], F32)]
         cu_win = [sbuf("cu_win0", [P, S + SPARE], F32), sbuf("cu_win1", [P, V + SPARE], F32)]
-        nc.vector.memset(cu_win[0][:, S:], 0.0)
         nc.vector.memset(cu_win[1][:, V:], 0.0)
         ident = sbuf("ident", [P, P], F32)
         make_identity(nc, ident[:])
@@ -84,12 +83,11 @@ def tile_picked_yhodge_tanh_p_kernel(
                 scale_all[32 * q : 32 * q + PASSES * SCALE_ROWS, :].bitcast(I32),
                 x_scales[:, SCALE_ROWS * q : SCALE_ROWS * (q + 1), :].bitcast(I32),
             )
-        nc.scalar.activation(y_win[0][:, S:], zeros[:], TANH)
-        w1_first = load_weight("w1", w1, 0)
-        w1_raw = {(0, 0): w1_first[:, :, 0:P], (0, 1): w1_first[:, :, P:N]}
-        w1_raw[1, 0] = load_weight("w1a", w1, 1, 0, P)[:]
+        nc.scalar.activation(cu_win[0][:, S:], zeros[:], TANH)
+        w1_raw = {(o, 0): load_weight("w1a", w1, o, 0, P)[:] for o in range(PASSES)}
         x_all.append(load_words(1))
-        w1_raw[1, 1] = load_weight("w1b", w1, 1, P, P)[:]
+        for o in range(PASSES):
+            w1_raw[o, 1] = load_weight("w1b", w1, o, P, P)[:]
         inc_t = load("inc_t", inc, U16)
         nc.sync.dma_start(sn_t[:], sn)
         w2_raw = [load_weight("w2", w2, o) for o in range(PASSES)]
@@ -147,7 +145,7 @@ def tile_picked_yhodge_tanh_p_kernel(
 
         pieces = [(0, HALF), (HALF, HALF + P), (HALF + P, S)]
         y0_acc = [bank("y0%d" % i, (0, 1, 7)[i], e1 - e0) for i, (e0, e1) in enumerate(pieces)]
-        y1_acc = bank("y1", 2, S)
+        y1_acc = [bank("y1%d" % i, (2, 5)[i], HALF) for i in range(2)]
         g1 = {}
         for o, b in ((0, 0), (1, 0), (0, 1), (1, 1)):
             g1[o, b] = sbuf("g1_%d%d" % (o, b), [P, P, PACK], BF16)
@@ -161,9 +159,11 @@ def tile_picked_yhodge_tanh_p_kernel(
             mx_pass(y0_acc[i][:], wq, 0, 1, e0, e1)
         for o in range(PASSES):
             wq = quantize("q1_%d1" % o, g1[o, 1][:], P)
-            mx_pass(y1_acc[:], wq, 0, o, 0, S)
+            for i, (e0, e1) in enumerate(halves):
+                mx_pass(y1_acc[i][:], wq, 0, o, e0, e1)
+        y_win.append(sbuf("y_win0", [P, S], F32, tag="w1b_raw1"))
         for i, (e0, e1) in enumerate(pieces):
-            copy = nc.scalar.copy if i == 0 else nc.vector.tensor_copy
+            copy = nc.vector.tensor_copy if i == 1 else nc.scalar.copy
             copy(y_win[0][:, e0:e1], y0_acc[i][:])
 
         li0 = sbuf("li0", [P, S], F32, tag="g1_11")
@@ -177,11 +177,13 @@ def tile_picked_yhodge_tanh_p_kernel(
                 wq = quantize("q%s%d%d" % (name, o, b), grouped[:, b * P : (b + 1) * P, :], P)
                 mx_pass(acc[b][:], wq, 0, o, 0, S)
 
-        fused(li[0], y_win[0], inc_t, 0, S, sn_t[:], MULT)
+        for e0, e1 in halves:
+            fused(li[0][:, e0:e1], y_win[0], inc_t, e0, e1, sn_t[:, e0:e1], MULT)
         h_acc = [bank("h%d" % b, 3 + b, S) for b in range(BLOCKS)]
         g2 = [g2_first[:], grouped_view(tail0[:])]
         y_win.append(sbuf("y_win1", [P, S], F32))
-        nc.scalar.copy(y_win[1][:], y1_acc[:])
+        for i, (e0, e1) in enumerate(halves):
+            nc.scalar.copy(y_win[1][:, e0:e1], y1_acc[i][:])
         for o in range(PASSES):
             interleave(g2[o], w2_raw[o], 0, N)
         for e0, e1 in halves:

@@ -76,8 +76,8 @@ def tile_picked_yhodge_tanh_p_kernel(
         sa_t = cu_win[0][:, 0:V]
         sb_t = cu_win[0][:, V:S]
 
-        offs_t = load("offs_t", offs, U16)
         x_all = [load_words(0)]
+        offs_t = load("offs_t", offs, U16)
         for q in range(4):
             nc.sync.dma_start(
                 scale_all[32 * q : 32 * q + PASSES * SCALE_ROWS, :].bitcast(I32),
@@ -93,12 +93,12 @@ def tile_picked_yhodge_tanh_p_kernel(
         w2_raw = [load_weight("w2", w2, o) for o in range(PASSES)]
         tail_t = load("tail_t", tail, U16)
         head_t = load("head_t", head, U16)
+        w3_last = shared.tile([P, PACK, N], F32, name="w3_last", offset=0)
+        w3_raw = [load_weight("w3", w3, 0), load_weight("w3", w3, 1, t=w3_last)]
         tri_t = load("tri_t", tri, U16)
         trj_t = load("trj_t", trj, U16)
         nc.sync.dma_start(sa_t, sa)
         nc.sync.dma_start(sb_t, sb)
-        w3_last = shared.tile([P, PACK, N], F32, name="w3_last", offset=0)
-        w3_raw = [load_weight("w3", w3, 0), load_weight("w3", w3, 1, t=w3_last)]
         face_t = load("face_t", face, U16)
         nc.sync.dma_start(sf_t, sf)
 
@@ -170,7 +170,7 @@ def tile_picked_yhodge_tanh_p_kernel(
         li1 = sbuf("li1", [P, S], F32)
         g2_first = sbuf("g2_first", [P, N, PACK], BF16, tag="q1_11_codes")
         li = [li0[:], li1[:]]
-        tail0 = sbuf("tail0", [P, S], F32)
+        late = sbuf("late", [P, S], F32)
 
         def quantize_blocks(name, grouped, acc, o):
             for b in range(BLOCKS):
@@ -180,20 +180,23 @@ def tile_picked_yhodge_tanh_p_kernel(
         for e0, e1 in halves:
             fused(li[0][:, e0:e1], y_win[0], inc_t, e0, e1, sn_t[:, e0:e1], MULT)
         h_acc = [bank("h%d" % b, 3 + b, S) for b in range(BLOCKS)]
-        g2 = [g2_first[:], grouped_view(tail0[:])]
+        g2 = [g2_first[:], grouped_view(late[:])]
         y_win.append(sbuf("y_win1", [P, S], F32))
         for i, (e0, e1) in enumerate(halves):
             nc.scalar.copy(y_win[1][:, e0:e1], y1_acc[i][:])
         for o in range(PASSES):
             interleave(g2[o], w2_raw[o], 0, N)
-        for e0, e1 in halves:
+        pairs = [li[b].rearrange("p (v d) -> p d v", d=2) for b in range(BLOCKS)]
+        for i, (e0, e1) in enumerate(pieces):
+            if i == 2:
+                nc.vector.tensor_tensor(dv_win[0][:, 0:V], pairs[0][:, 0, :], pairs[0][:, 1, :], ADD)
             fused(li[1][:, e0:e1], y_win[1], inc_t, e0, e1, sn_t[:, e0:e1], MULT)
         wq = quantize("qh0", g2[0], N)
         for b in range(BLOCKS):
             mx_pass(h_acc[b][:], wq, b * P, 0, 0, S)
-        for b in range(BLOCKS):
-            pairs = li[b].rearrange("p (v d) -> p d v", d=2)
-            nc.vector.tensor_tensor(dv_win[b][:, 0:V], pairs[:, 0, :], pairs[:, 1, :], ADD)
+        tail0 = [sbuf("tail0a", [P, HALF], F32)[:], late[:, 0:HALF]]
+        down0 = [late[:, HALF:S], sbuf("down0b", [P, HALF], F32)[:]]
+        nc.vector.tensor_copy(tail0[0], dv_win[0][:].indirect(cols(tail_t, 0, HALF)))
         quantize_blocks("h", g2[1], h_acc, 1)
         g3 = [sbuf("g3_%d" % o, [P, N, PACK], BF16) for o in range(PASSES)]
         for o in range(PASSES):
@@ -202,11 +205,9 @@ def tile_picked_yhodge_tanh_p_kernel(
             h_win.append(shared.tile([P, S], F32, name="h_win%d" % b, offset=b * S * 4))
         for b in range(BLOCKS):
             nc.scalar.copy(h_win[b][:], h_acc[b][:])
-        for e0, e1 in halves:
-            nc.vector.tensor_copy(tail0[:, e0:e1], dv_win[0][:].indirect(cols(tail_t, e0, e1)))
-        down0 = sbuf("down0", [P, S], F32)
-        fused(down0[:, 0:HALF], dv_win[0], head_t, 0, HALF, tail0[:, 0:HALF], SUB)
-        fused(down0[:, HALF:S], dv_win[0], head_t, HALF, S, tail0[:, HALF:S], SUB)
+        nc.vector.tensor_copy(tail0[1], dv_win[0][:].indirect(cols(tail_t, HALF, S)))
+        for i, (e0, e1) in enumerate(halves):
+            fused(down0[i], dv_win[0], head_t, e0, e1, tail0[i], SUB)
 
         sides = [sbuf("sides0", [P, 2 * V], F32), sbuf("sides1", [P, 2 * V], F32)]
         own = [bank("own%d" % b, 5 + b, S) for b in range(BLOCKS)]
@@ -220,6 +221,23 @@ def tile_picked_yhodge_tanh_p_kernel(
         fused(sides[1][:, V:], h_win[1], trj_t, 0, V, sb_t, MULT)
         own0 = sbuf("own0", [P, S], F32)
         nc.scalar.copy(own0[:], own[0][:])
+        dv1_sum = bank("dv1_sum", 4, V)
+        for d in range(2):
+            for c in range(2):
+                nc.tensor.matmul(
+                    dv1_sum[:, c * P : (c + 1) * P],
+                    pairs[1][:, d, c * P : (c + 1) * P],
+                    ident[:],
+                    start=d == 0 and c == 0,
+                    stop=d == 1 and c == 1,
+                    is_transpose=True,
+                )
+        dv1_turned = sbuf("dv1_turned", [P, V], F32)
+        nc.scalar.copy(dv1_turned[:], dv1_sum[:])
+        dv1_back = bank("dv1_back", 7, V)
+        for c in range(2):
+            nc.tensor.transpose(dv1_back[:, c * P : (c + 1) * P], dv1_turned[:, c * P : (c + 1) * P], ident[:])
+        nc.scalar.copy(dv_win[1][:, 0:V], dv1_back[:])
         for b in range(BLOCKS):
             nc.vector.tensor_tensor(cu_win[b][:, 0:V], sides[b][:, 0:V], sides[b][:, V:], ADD)
 
@@ -231,19 +249,18 @@ def tile_picked_yhodge_tanh_p_kernel(
         def add_term(term, first=False, last=False):
             for i in range(2):
                 for c in range(2):
-                    e0 = i * HALF + c * P
                     nc.tensor.matmul(
                         sums[i][:, c * P : (c + 1) * P],
-                        term[:, e0 : e0 + P],
+                        term[i][:, c * P : (c + 1) * P],
                         ident[:],
                         start=first and c == 0,
                         stop=last and c == 1,
                         is_transpose=True,
                     )
 
-        add_term(down0[:], first=True)
-        add_term(own0[:])
-        add_term(up0[:], last=True)
+        add_term(down0, first=True)
+        add_term([own0[:, e0:e1] for e0, e1 in halves])
+        add_term([up0[:, e0:e1] for e0, e1 in halves], last=True)
         backs = []
         for i in range(2):
             turned = sbuf("turned%d" % i, [P, HALF], F32)

@@ -149,7 +149,7 @@ def tile_picked_yhodge_tanh_p_kernel(
         g1 = {}
         for o, b in ((0, 0), (1, 0), (0, 1), (1, 1)):
             g1[o, b] = sbuf("g1_%d%d" % (o, b), [P, P, PACK], BF16)
-            interleave(g1[o, b][:], w1_raw[o, b], 0, P)
+            interleave(g1[o, b][:], w1_raw[o, b], 0, P, nc.vector.tensor_copy if (o, b) == (1, 1) else nc.scalar.copy)
         wq = quantize("q1_00", g1[0, 0][:], P)
         for i, (e0, e1) in enumerate(pieces):
             mx_pass(y0_acc[i][:], wq, 0, 0, e0, e1)
@@ -161,10 +161,9 @@ def tile_picked_yhodge_tanh_p_kernel(
             wq = quantize("q1_%d1" % o, g1[o, 1][:], P)
             for i, (e0, e1) in enumerate(halves):
                 mx_pass(y1_acc[i][:], wq, 0, o, e0, e1)
-        y_win.append(sbuf("y_win0", [P, S], F32, tag="w1b_raw1"))
+        y_win.append(sbuf("y_win0", [P, S], F32, tag="w1b_raw0"))
         for i, (e0, e1) in enumerate(pieces):
-            copy = nc.vector.tensor_copy if i == 1 else nc.scalar.copy
-            copy(y_win[0][:, e0:e1], y0_acc[i][:])
+            nc.scalar.copy(y_win[0][:, e0:e1], y0_acc[i][:])
 
         li0 = sbuf("li0", [P, S], F32, tag="g1_11")
         li1 = sbuf("li1", [P, S], F32)
@@ -283,7 +282,7 @@ def tile_picked_yhodge_tanh_p_kernel(
             nc.vector.tensor_tensor(rest1[:, e0:e1], own[1][:, e0:e1], up1[:, e0:e1], ADD)
         for e0, e1 in halves:
             fused(plus1[:, e0:e1], dv_win[1], head_t, e0, e1, rest1[:, e0:e1], ADD)
-        for e0, e1 in ((0, HALF), (HALF, HALF + P), (HALF + P, S)):
+        for e0, e1 in pieces:
             neg = sbuf("neg%d" % e0, [P, e1 - e0], F32)
             fused(neg[:], dv_win[1], tail_t, e0, e1, plus1[:, e0:e1], SUB)
             res = sbuf("res1%d" % e0, [P, e1 - e0], F32)

@@ -84,8 +84,9 @@ def tile_picked_yhodge_tanh_p_kernel(
                 x_scales[:, SCALE_ROWS * q : SCALE_ROWS * (q + 1), :].bitcast(I32),
             )
         nc.scalar.activation(cu_win[0][:, S:], zeros[:], TANH)
-        w1_raw = {(o, 0): load_weight("w1a", w1, o, 0, P)[:] for o in range(PASSES)}
+        w1_raw = {(0, 0): load_weight("w1a", w1, 0, 0, P)[:]}
         x_all.append(load_words(1))
+        w1_raw[1, 0] = load_weight("w1a", w1, 1, 0, P)[:]
         for o in range(PASSES):
             w1_raw[o, 1] = load_weight("w1b", w1, o, P, P)[:]
         inc_t = load("inc_t", inc, U16)

@@ -60,21 +60,20 @@ def tile_picked_yhodge_tanh_p_kernel(
             nc.sync.dma_start(t[:], rows.rearrange("(p t) c -> p t c", t=PACK))
             return t
 
+        def at(name, shape, dtype, word):
+            return shared.tile(shape, dtype, name=name, offset=4 * word, align_bytes=64)
+
+        RAW1, RAW2 = 0, 4 * S
+        W1_SLOT = {(1, 0): 0, (0, 0): 1, (0, 1): 2, (1, 1): 3}
+        RAW3 = [8 * S, 10 * S]
+
         scale_all = sbuf("scale_all", [P, T], U8)
         nc.gpsimd.memset(scale_all[:].bitcast(I32), 0)
         zeros = sbuf("zeros", [P, SPARE], F32)
         nc.vector.memset(zeros[:], 0.0)
-        y_win = []
-        h_win = []
-        dv_win = [sbuf("dv_win0", [P, S], F32), sbuf("dv_win1", [P, V + S], F32)]
-        cu_win = [sbuf("cu_win0", [P, S + SPARE], F32), sbuf("cu_win1", [P, V + SPARE], F32)]
-        nc.vector.memset(cu_win[1][:, V:], 0.0)
-        ident = sbuf("ident", [P, P], F32)
-        make_identity(nc, ident[:])
-        sn_t = dv_win[0]
-        sf_t = dv_win[1][:, V:]
-        sa_t = cu_win[0][:, 0:V]
-        sb_t = cu_win[0][:, V:S]
+        dv_win1 = sbuf("dv_win1", [P, V + S], F32)
+        sf_t = dv_win1[:, V:]
+        cu_win1 = sbuf("cu_win1", [P, V + SPARE], F32)
 
         x_all = [load_words(0)]
         offs_t = load("offs_t", offs, U16)
@@ -83,23 +82,30 @@ def tile_picked_yhodge_tanh_p_kernel(
                 scale_all[32 * q : 32 * q + PASSES * SCALE_ROWS, :].bitcast(I32),
                 x_scales[:, SCALE_ROWS * q : SCALE_ROWS * (q + 1), :].bitcast(I32),
             )
-        nc.scalar.activation(cu_win[0][:, S:], zeros[:], TANH)
-        w1_raw = {(0, 0): load_weight("w1a", w1, 0, 0, P)[:]}
+        nc.scalar.activation(cu_win1[:, V:], zeros[:], TANH)
+        ident = sbuf("ident", [P, P], F32)
+        make_identity(nc, ident[:])
+        w1_raw = {}
+
+        def load_w1(o, b):
+            t = at("w1_raw%d%d" % (o, b), [P, PACK, P], F32, RAW1 + W1_SLOT[o, b] * S)
+            w1_raw[o, b] = load_weight("w1", w1, o, b * P, P, t=t)
+
+        load_w1(0, 0)
         x_all.append(load_words(1))
-        w1_raw[1, 0] = load_weight("w1a", w1, 1, 0, P)[:]
-        for o in range(PASSES):
-            w1_raw[o, 1] = load_weight("w1b", w1, o, P, P)[:]
+        load_w1(1, 0)
+        load_w1(0, 1)
+        load_w1(1, 1)
         inc_t = load("inc_t", inc, U16)
-        nc.sync.dma_start(sn_t[:], sn)
-        w2_raw = [load_weight("w2", w2, o) for o in range(PASSES)]
+        sn_t = load("sn_t", sn, F32)
+        w2_raw = [load_weight("w2", w2, 1 - o, t=at("w2_raw%d" % o, [P, PACK, N], F32, RAW2 + o * 2 * S)) for o in range(PASSES)]
         tail_t = load("tail_t", tail, U16)
         head_t = load("head_t", head, U16)
-        w3_last = shared.tile([P, PACK, N], F32, name="w3_last", offset=0)
-        w3_raw = [load_weight("w3", w3, 0), load_weight("w3", w3, 1, t=w3_last)]
+        w3_raw = [load_weight("w3", w3, 1 - o, t=at("w3_raw%d" % o, [P, PACK, N], F32, RAW3[o])) for o in range(PASSES)]
         tri_t = load("tri_t", tri, U16)
         trj_t = load("trj_t", trj, U16)
-        nc.sync.dma_start(sa_t, sa)
-        nc.sync.dma_start(sb_t, sb)
+        sa_t = load("sa_t", sa, F32)
+        sb_t = load("sb_t", sb, F32)
         face_t = load("face_t", face, U16)
         nc.sync.dma_start(sf_t, sf)
 
@@ -107,13 +113,19 @@ def tile_picked_yhodge_tanh_p_kernel(
             return lst[:, e0 // 16 : e1 // 16]
 
         halves = [(0, HALF), (HALF, S)]
-        x_pick = [sbuf("x_pick%d" % o, [P, S], U32) for o in range(PASSES)]
+        x_pick0 = sbuf("x_pick0", [P, S], U32)
+        x_pick1 = [sbuf("x_pick1a", [P, HALF], U32), at("x_pick1b", [P, HALF], U32, RAW1)]
+
+        def picked(o, e0, e1):
+            if o == 0:
+                return x_pick0[:, e0:e1]
+            i = e0 // HALF
+            return x_pick1[i][:, e0 - i * HALF : e1 - i * HALF]
+
         scale_pick = sbuf("scale_pick", [P, S], U8)
-        nc.vector.tensor_copy(x_pick[0][:], x_all[0].indirect(offs_t[:]))
+        nc.vector.tensor_copy(x_pick0[:], x_all[0].indirect(offs_t[:]))
         nc.vector.tensor_copy(scale_pick[:], scale_all[:].indirect(offs_t[:]))
 
-        def grouped_view(words):
-            return words.bitcast(BF16).rearrange("p (c t) -> p c t", t=PACK)
 
         def interleave(dst, raw, c0, width, copy=nc.scalar.copy):
             copy(
@@ -121,125 +133,130 @@ def tile_picked_yhodge_tanh_p_kernel(
                 raw[:, :, c0 : c0 + width].rearrange("p t (c i) -> p c t i", i=4),
             )
 
-        def quantize(name, grouped, width):
-            codes = sbuf(name + "_codes", [P, width], U32, tag=name + "_codes")
+        def quantize(name, grouped, width, codes=None):
+            if codes is None:
+                codes = sbuf(name + "_codes", [P, width], U32)
             scales = sbuf(name + "_scales", [P, width], U8)
             nc.vector.quantize_mx(
                 out=codes[:].bitcast(FP8X4), scales=scales[:], in_=grouped.rearrange("p c t -> p (c t)")
             )
             return codes, scales
 
-        def mx_pass(acc, wq, c0, o, e0, e1):
+        def mx_pass(acc, wq, c0, o, e0, e1, start, stop):
             codes, scales = wq
             nc.tensor.matmul_mx(
                 out=acc,
                 lhsT=codes[:, c0 : c0 + P].bitcast(FP8X4),
                 lhsT_scale=scales[:, c0 : c0 + P],
-                rhs=x_pick[o][:, e0:e1].bitcast(FP8X4),
+                rhs=picked(o, e0, e1).bitcast(FP8X4),
                 rhs_scale=scale_pick[SCALE_ROWS * o :, e0:e1],
-                start=o == 0,
-                stop=o == PASSES - 1,
+                start=start,
+                stop=stop,
             )
+
+        def open_wide(acc, wq, c0):
+            for i, (e0, e1) in enumerate(halves):
+                mx_pass(acc[:, e0:e1], wq, c0, 1, e0, e1, i == 0, False)
+
+        def close_wide(acc, wq, c0):
+            mx_pass(acc[:], wq, c0, 0, 0, S, False, True)
 
         def fused(dst, window, lst, e0, e1, other, op):
             nc.vector.tensor_tensor(dst, window[:].indirect(cols(lst, e0, e1)), other, op)
 
+        def add_turned(name, terms, sum_bank, turned):
+            acc = bank(name + "_sum", sum_bank, V)
+            for d in range(2):
+                for c in range(2):
+                    nc.tensor.matmul(
+                        acc[:, c * P : (c + 1) * P],
+                        terms[d][:, c * P : (c + 1) * P],
+                        ident[:],
+                        start=d == 0 and c == 0,
+                        stop=d == 1 and c == 1,
+                        is_transpose=True,
+                    )
+            nc.scalar.copy(turned[:], acc[:])
+
+        def turn_back(name, turned, back_bank, dst):
+            back = bank(name + "_back", back_bank, V)
+            for c in range(2):
+                nc.tensor.transpose(back[:, c * P : (c + 1) * P], turned[:, c * P : (c + 1) * P], ident[:])
+            nc.scalar.copy(dst, back[:])
+
         pieces = [(0, HALF), (HALF, HALF + P), (HALF + P, S)]
         y0_acc = [bank("y0%d" % i, (0, 1, 7)[i], e1 - e0) for i, (e0, e1) in enumerate(pieces)]
         y1_acc = [bank("y1%d" % i, (2, 5)[i], HALF) for i in range(2)]
-        g1 = {}
-        for o, b in ((0, 0), (1, 0), (0, 1), (1, 1)):
-            g1[o, b] = sbuf("g1_%d%d" % (o, b), [P, P, PACK], BF16)
-            interleave(g1[o, b][:], w1_raw[o, b], 0, P, nc.vector.tensor_copy if (o, b) == (1, 1) else nc.scalar.copy)
-        wq = quantize("q1_00", g1[0, 0][:], P)
+        g1 = [sbuf("g1_%d" % b, [P, PASSES * P, PACK], BF16) for b in range(BLOCKS)]
+        for b in range(BLOCKS):
+            for o in range(PASSES):
+                interleave(g1[b][:, o * P : (o + 1) * P, :], w1_raw[o, b], 0, P)
+        wq = quantize("q1_00", g1[0][:, 0:P, :], P)
         for i, (e0, e1) in enumerate(pieces):
-            mx_pass(y0_acc[i][:], wq, 0, 0, e0, e1)
-        wq = quantize("q1_10", g1[1, 0][:], P)
+            mx_pass(y0_acc[i][:], wq, 0, 0, e0, e1, True, False)
+        wq = quantize("q1_01", g1[0][:, P:, :], P)
         for i, (e0, e1) in enumerate(pieces):
-            nc.vector.tensor_copy(x_pick[1][:, e0:e1], x_all[1].indirect(cols(offs_t, e0, e1)))
-            mx_pass(y0_acc[i][:], wq, 0, 1, e0, e1)
+            nc.vector.tensor_copy(picked(1, e0, e1), x_all[1].indirect(cols(offs_t, e0, e1)))
+            mx_pass(y0_acc[i][:], wq, 0, 1, e0, e1, False, True)
         for o in range(PASSES):
-            wq = quantize("q1_%d1" % o, g1[o, 1][:], P)
+            wq = quantize("q1_1%d" % o, g1[1][:, o * P : (o + 1) * P, :], P)
             for i, (e0, e1) in enumerate(halves):
-                mx_pass(y1_acc[i][:], wq, 0, o, e0, e1)
-        y_win.append(sbuf("y_win0", [P, S], F32, tag="w1b_raw0"))
+                mx_pass(y1_acc[i][:], wq, 0, o, e0, e1, o == 0, o == 1)
+        y_win = [at("y_win0", [P, S + SPARE], F32, RAW1 + 2 * S + SPARE), at("y_win1", [P, S + SPARE], F32, RAW1 + S)]
         for i, (e0, e1) in enumerate(pieces):
             nc.scalar.copy(y_win[0][:, e0:e1], y0_acc[i][:])
-
-        li0 = sbuf("li0", [P, S], F32, tag="g1_11")
-        li1 = sbuf("li1", [P, S], F32)
-        g2_first = sbuf("g2_first", [P, N, PACK], BF16, tag="q1_11_codes")
-        li = [li0[:], li1[:]]
-        late = sbuf("late", [P, S], F32)
-
-        def quantize_blocks(name, grouped, acc, o):
-            for b in range(BLOCKS):
-                wq = quantize("q%s%d%d" % (name, o, b), grouped[:, b * P : (b + 1) * P, :], P)
-                mx_pass(acc[b][:], wq, 0, o, 0, S)
-
-        for e0, e1 in halves:
-            fused(li[0][:, e0:e1], y_win[0], inc_t, e0, e1, sn_t[:, e0:e1], MULT)
-        h_acc = [bank("h%d" % b, 3 + b, S) for b in range(BLOCKS)]
-        g2 = [g2_first[:], grouped_view(late[:])]
-        y_win.append(sbuf("y_win1", [P, S], F32))
         for i, (e0, e1) in enumerate(halves):
             nc.scalar.copy(y_win[1][:, e0:e1], y1_acc[i][:])
-        for o in range(PASSES):
-            interleave(g2[o], w2_raw[o], 0, N)
-        pairs = [li[b].rearrange("p (v d) -> p d v", d=2) for b in range(BLOCKS)]
-        for i, (e0, e1) in enumerate(pieces):
-            if i == 2:
-                nc.vector.tensor_tensor(dv_win[0][:, 0:V], pairs[0][:, 0, :], pairs[0][:, 1, :], ADD)
-            fused(li[1][:, e0:e1], y_win[1], inc_t, e0, e1, sn_t[:, e0:e1], MULT)
-        wq = quantize("qh0", g2[0], N)
+        li = [sbuf("li%d" % b, [P, S], F32) for b in range(BLOCKS)]
         for b in range(BLOCKS):
-            mx_pass(h_acc[b][:], wq, b * P, 0, 0, S)
-        tail0 = [sbuf("tail0a", [P, HALF], F32)[:], late[:, 0:HALF]]
-        down0 = [late[:, HALF:S], sbuf("down0b", [P, HALF], F32)[:]]
-        nc.vector.tensor_copy(tail0[0], dv_win[0][:].indirect(cols(tail_t, 0, HALF)))
-        quantize_blocks("h", g2[1], h_acc, 1)
-        g3 = [sbuf("g3_%d" % o, [P, N, PACK], BF16) for o in range(PASSES)]
-        for o in range(PASSES):
-            interleave(g3[o][:], w3_raw[o], 0, N)
+            fused(li[b][:], y_win[b], inc_t, 0, S, sn_t[:], MULT)
+        pairs = [li[b][:].rearrange("p (v d) -> p d v", d=2) for b in range(BLOCKS)]
+
+        h_acc = [bank("h%d" % b, 3 + b, S) for b in range(BLOCKS)]
+        g2 = [sbuf("g2_%d" % o, [P, N, PACK], BF16) for o in range(PASSES)]
+        interleave(g2[0][:], w2_raw[0], 0, N)
         for b in range(BLOCKS):
-            h_win.append(shared.tile([P, S], F32, name="h_win%d" % b, offset=b * S * 4))
+            interleave(g2[1][:, b * P : (b + 1) * P, :], w2_raw[1], b * P, P)
+        dv_win0 = at("dv_win0", [P, 2 * S], F32, RAW2)
+        nc.vector.tensor_tensor(dv_win0[:, 0:V], pairs[0][:, 0, :], pairs[0][:, 1, :], ADD)
+        wq = quantize("q2_0", g2[0][:], N)
+        for b in range(BLOCKS):
+            open_wide(h_acc[b], wq, b * P)
+        for b in range(BLOCKS):
+            wq = quantize(
+                "q2_1%d" % b, g2[1][:, b * P : (b + 1) * P, :], P
+            )
+            close_wide(h_acc[b], wq, 0)
+        tail0 = at("tail0", [P, S], F32, RAW2 + 2 * S)
+        nc.vector.tensor_copy(tail0[:], dv_win0[:].indirect(tail_t[:]))
+        g3 = [sbuf("g3_0", [P, N, PACK], BF16), sbuf("g3_1", [P, N, PACK], BF16)]
+        own = [bank("own%d" % b, 5 + b, S) for b in range(BLOCKS)]
+        interleave(g3[0][:], w3_raw[0], 0, N)
+        wq = quantize("q3_0", g3[0][:], N)
+        for b in range(BLOCKS):
+            open_wide(own[b], wq, b * P)
+        down0 = at("down0", [P, S], F32, RAW3[0])
+        fused(down0[:], dv_win0, head_t, 0, S, tail0[:], SUB)
+        interleave(g3[1][:], w3_raw[1], 0, N)
+        wq = quantize("q3_1", g3[1][:], N)
+        for b in range(BLOCKS):
+            close_wide(own[b], wq, b * P)
+        h_win = [at("h_win%d" % b, [P, S], F32, RAW3[1] + b * S) for b in range(BLOCKS)]
         for b in range(BLOCKS):
             nc.scalar.copy(h_win[b][:], h_acc[b][:])
-        nc.vector.tensor_copy(tail0[1], dv_win[0][:].indirect(cols(tail_t, HALF, S)))
-        for i, (e0, e1) in enumerate(halves):
-            fused(down0[i], dv_win[0], head_t, e0, e1, tail0[i], SUB)
 
-        sides = [sbuf("sides0", [P, 2 * V], F32), sbuf("sides1", [P, 2 * V], F32)]
-        own = [bank("own%d" % b, 5 + b, S) for b in range(BLOCKS)]
-        for o in range(PASSES):
-            wq = quantize("qown%d" % o, g3[o][:], N)
-            for b in range(BLOCKS):
-                mx_pass(own[b][:], wq, b * P, o, 0, S)
-        fused(sides[0][:, 0:V], h_win[0], tri_t, 0, V, sa_t, MULT)
-        fused(sides[0][:, V:], h_win[0], trj_t, 0, V, sb_t, MULT)
-        fused(sides[1][:, 0:V], h_win[1], tri_t, 0, V, sa_t, MULT)
-        fused(sides[1][:, V:], h_win[1], trj_t, 0, V, sb_t, MULT)
-        own0 = sbuf("own0", [P, S], F32)
-        nc.scalar.copy(own0[:], own[0][:])
-        dv1_sum = bank("dv1_sum", 4, V)
-        for d in range(2):
-            for c in range(2):
-                nc.tensor.matmul(
-                    dv1_sum[:, c * P : (c + 1) * P],
-                    pairs[1][:, d, c * P : (c + 1) * P],
-                    ident[:],
-                    start=d == 0 and c == 0,
-                    stop=d == 1 and c == 1,
-                    is_transpose=True,
-                )
-        dv1_turned = sbuf("dv1_turned", [P, V], F32)
-        nc.scalar.copy(dv1_turned[:], dv1_sum[:])
-        dv1_back = bank("dv1_back", 7, V)
-        for c in range(2):
-            nc.tensor.transpose(dv1_back[:, c * P : (c + 1) * P], dv1_turned[:, c * P : (c + 1) * P], ident[:])
-        nc.scalar.copy(dv_win[1][:, 0:V], dv1_back[:])
+        sides = [sbuf("sides%d" % b, [P, 2 * V], F32) for b in range(BLOCKS)]
+        cu_win = [at("cu_win0", [P, S + SPARE], F32, RAW2), cu_win1]
+        for b in range(BLOCKS):
+            fused(sides[b][:, 0:V], h_win[b], tri_t, 0, V, sa_t[:], MULT)
+            fused(sides[b][:, V:], h_win[b], trj_t, 0, V, sb_t[:], MULT)
         for b in range(BLOCKS):
             nc.vector.tensor_tensor(cu_win[b][:, 0:V], sides[b][:, 0:V], sides[b][:, V:], ADD)
+        dv1_turned = sbuf("dv1_turned", [P, V], F32)
+        add_turned("dv1", [pairs[1][:, d, :] for d in range(2)], 4, dv1_turned)
+        turn_back("dv1", dv1_turned, 7, dv_win1[:, 0:V])
+        own0 = sbuf("own0", [P, S], F32)
+        nc.scalar.copy(own0[:], own[0][:])
 
         up0 = sbuf("up0", [P, S], F32)
         fused(up0[:], cu_win[0], face_t, 0, S, sf_t, MULT)
@@ -247,11 +264,11 @@ def tile_picked_yhodge_tanh_p_kernel(
         sums = [bank("sum%d" % i, i, HALF) for i in range(2)]
 
         def add_term(term, first=False, last=False):
-            for i in range(2):
+            for i, (e0, e1) in enumerate(halves):
                 for c in range(2):
                     nc.tensor.matmul(
                         sums[i][:, c * P : (c + 1) * P],
-                        term[i][:, c * P : (c + 1) * P],
+                        term[:, e0 + c * P : e0 + (c + 1) * P],
                         ident[:],
                         start=first and c == 0,
                         stop=last and c == 1,
@@ -259,8 +276,8 @@ def tile_picked_yhodge_tanh_p_kernel(
                     )
 
         add_term(down0, first=True)
-        add_term([own0[:, e0:e1] for e0, e1 in halves])
-        add_term([up0[:, e0:e1] for e0, e1 in halves], last=True)
+        add_term(own0)
+        add_term(up0, last=True)
         backs = []
         for i in range(2):
             turned = sbuf("turned%d" % i, [P, HALF], F32)
@@ -282,10 +299,10 @@ def tile_picked_yhodge_tanh_p_kernel(
         for e0, e1 in halves:
             nc.vector.tensor_tensor(rest1[:, e0:e1], own[1][:, e0:e1], up1[:, e0:e1], ADD)
         for e0, e1 in halves:
-            fused(plus1[:, e0:e1], dv_win[1], head_t, e0, e1, rest1[:, e0:e1], ADD)
+            fused(plus1[:, e0:e1], dv_win1, head_t, e0, e1, rest1[:, e0:e1], ADD)
         for e0, e1 in pieces:
             neg = sbuf("neg%d" % e0, [P, e1 - e0], F32)
-            fused(neg[:], dv_win[1], tail_t, e0, e1, plus1[:, e0:e1], SUB)
+            fused(neg[:], dv_win1, tail_t, e0, e1, plus1[:, e0:e1], SUB)
             res = sbuf("res1%d" % e0, [P, e1 - e0], F32)
             nc.scalar.activation(res[:], neg[:], TANH, scale=-1.0)
             nc.sync.dma_start(out[P : 2 * P, e0:e1], res[:])

@@ -64,15 +64,16 @@ def tile_picked_yhodge_tanh_p_kernel(
             return shared.tile(shape, dtype, name=name, offset=4 * word, align_bytes=64)
 
         RAW1, RAW2 = 0, 4 * S
-        W1_SLOT = {(1, 0): 0, (0, 0): 1, (0, 1): 2, (1, 1): 3}
+        W1_SLOT = {(0, 0): 0, (1, 0): 1, (0, 1): 2, (1, 1): 3}
         RAW3 = [8 * S, 10 * S]
 
         scale_all = sbuf("scale_all", [P, T], U8)
         nc.gpsimd.memset(scale_all[:].bitcast(I32), 0)
         zeros = sbuf("zeros", [P, SPARE], F32)
         nc.vector.memset(zeros[:], 0.0)
-        dv_win1 = sbuf("dv_win1", [P, V + S], F32)
-        sf_t = dv_win1[:, V:]
+        dv_win1 = sbuf("dv_win1", [P, 2 * S], F32)
+        sf_t = dv_win1[:, V : V + S]
+        sa_t = dv_win1[:, V + S :]
         cu_win1 = sbuf("cu_win1", [P, V + SPARE], F32)
 
         x_all = [load_words(0)]
@@ -98,13 +99,13 @@ def tile_picked_yhodge_tanh_p_kernel(
         load_w1(1, 1)
         inc_t = load("inc_t", inc, U16)
         sn_t = load("sn_t", sn, F32)
-        w2_raw = [load_weight("w2", w2, 1 - o, t=at("w2_raw%d" % o, [P, PACK, N], F32, RAW2 + o * 2 * S)) for o in range(PASSES)]
+        w2_raw = [load_weight("w2", w2, o, t=at("w2_raw%d" % o, [P, PACK, N], F32, RAW2 + o * 2 * S)) for o in range(PASSES)]
         tail_t = load("tail_t", tail, U16)
         head_t = load("head_t", head, U16)
-        w3_raw = [load_weight("w3", w3, 1 - o, t=at("w3_raw%d" % o, [P, PACK, N], F32, RAW3[o])) for o in range(PASSES)]
+        w3_raw = [load_weight("w3", w3, o, t=at("w3_raw%d" % o, [P, PACK, N], F32, RAW3[o])) for o in range(PASSES)]
         tri_t = load("tri_t", tri, U16)
         trj_t = load("trj_t", trj, U16)
-        sa_t = load("sa_t", sa, F32)
+        nc.sync.dma_start(sa_t, sa)
         sb_t = load("sb_t", sb, F32)
         face_t = load("face_t", face, U16)
         nc.sync.dma_start(sf_t, sf)
@@ -113,17 +114,13 @@ def tile_picked_yhodge_tanh_p_kernel(
             return lst[:, e0 // 16 : e1 // 16]
 
         halves = [(0, HALF), (HALF, S)]
-        x_pick0 = sbuf("x_pick0", [P, S], U32)
-        x_pick1 = [sbuf("x_pick1a", [P, HALF], U32), at("x_pick1b", [P, HALF], U32, RAW1)]
+        x_pick = [sbuf("x_pick0", [P, S], U32), sbuf("x_pick1", [P, S], U32)]
 
         def picked(o, e0, e1):
-            if o == 0:
-                return x_pick0[:, e0:e1]
-            i = e0 // HALF
-            return x_pick1[i][:, e0 - i * HALF : e1 - i * HALF]
+            return x_pick[o][:, e0:e1]
 
         scale_pick = sbuf("scale_pick", [P, S], U8)
-        nc.vector.tensor_copy(x_pick0[:], x_all[0].indirect(offs_t[:]))
+        nc.vector.tensor_copy(x_pick[0][:], x_all[0].indirect(offs_t[:]))
         nc.vector.tensor_copy(scale_pick[:], scale_all[:].indirect(offs_t[:]))
 
 
@@ -135,10 +132,10 @@ def tile_picked_yhodge_tanh_p_kernel(
 
         def quantize(name, grouped, width, codes=None):
             if codes is None:
-                codes = sbuf(name + "_codes", [P, width], U32)
+                codes = sbuf(name + "_codes", [P, width], U32)[:]
             scales = sbuf(name + "_scales", [P, width], U8)
             nc.vector.quantize_mx(
-                out=codes[:].bitcast(FP8X4), scales=scales[:], in_=grouped.rearrange("p c t -> p (c t)")
+                out=codes.bitcast(FP8X4), scales=scales[:], in_=grouped.rearrange("p c t -> p (c t)")
             )
             return codes, scales
 
@@ -155,11 +152,10 @@ def tile_picked_yhodge_tanh_p_kernel(
             )
 
         def open_wide(acc, wq, c0):
-            for i, (e0, e1) in enumerate(halves):
-                mx_pass(acc[:, e0:e1], wq, c0, 1, e0, e1, i == 0, False)
+            mx_pass(acc[:], wq, c0, 0, 0, S, True, False)
 
         def close_wide(acc, wq, c0):
-            mx_pass(acc[:], wq, c0, 0, 0, S, False, True)
+            mx_pass(acc[:], wq, c0, 1, 0, S, False, True)
 
         def fused(dst, window, lst, e0, e1, other, op):
             nc.vector.tensor_tensor(dst, window[:].indirect(cols(lst, e0, e1)), other, op)
@@ -185,83 +181,88 @@ def tile_picked_yhodge_tanh_p_kernel(
             nc.scalar.copy(dst, back[:])
 
         pieces = [(0, HALF), (HALF, HALF + P), (HALF + P, S)]
-        y0_acc = [bank("y0%d" % i, (0, 1, 7)[i], e1 - e0) for i, (e0, e1) in enumerate(pieces)]
+        y0_acc = [bank("y0%d" % i, i, HALF) for i in range(2)]
         y1_acc = [bank("y1%d" % i, (2, 5)[i], HALF) for i in range(2)]
-        g1 = [sbuf("g1_%d" % b, [P, PASSES * P, PACK], BF16) for b in range(BLOCKS)]
-        for b in range(BLOCKS):
-            for o in range(PASSES):
-                interleave(g1[b][:, o * P : (o + 1) * P, :], w1_raw[o, b], 0, P)
-        wq = quantize("q1_00", g1[0][:, 0:P, :], P)
-        for i, (e0, e1) in enumerate(pieces):
+        g1a = sbuf("g1a", [P, PASSES * P, PACK], BF16)
+        g1b = [sbuf("g1b%d" % o, [P, P, PACK], BF16) for o in range(PASSES)]
+        for o in range(PASSES):
+            interleave(g1a[:, o * P : (o + 1) * P, :], w1_raw[o, 0], 0, P)
+        interleave(g1b[0][:], w1_raw[0, 1], 0, P)
+        codes_a = sbuf("codes_a", [P, PASSES * P], U32)
+        wq = quantize("q1_00", g1a[:, 0:P, :], P, codes=codes_a[:, 0:P])
+        for i, (e0, e1) in enumerate(halves):
             mx_pass(y0_acc[i][:], wq, 0, 0, e0, e1, True, False)
-        wq = quantize("q1_01", g1[0][:, P:, :], P)
-        for i, (e0, e1) in enumerate(pieces):
-            nc.vector.tensor_copy(picked(1, e0, e1), x_all[1].indirect(cols(offs_t, e0, e1)))
+        nc.vector.tensor_copy(x_pick[1][:], x_all[1].indirect(offs_t[:]))
+        wq = quantize("q1_01", g1a[:, P:, :], P, codes=codes_a[:, P:])
+        for i, (e0, e1) in enumerate(halves):
             mx_pass(y0_acc[i][:], wq, 0, 1, e0, e1, False, True)
         for o in range(PASSES):
-            wq = quantize("q1_1%d" % o, g1[1][:, o * P : (o + 1) * P, :], P)
+            if o == 1:
+                interleave(g1b[1][:], w1_raw[1, 1], 0, P, nc.vector.tensor_copy)
+            wq = quantize("q1_1%d" % o, g1b[o][:], P)
             for i, (e0, e1) in enumerate(halves):
                 mx_pass(y1_acc[i][:], wq, 0, o, e0, e1, o == 0, o == 1)
-        y_win = [at("y_win0", [P, S + SPARE], F32, RAW1 + 2 * S + SPARE), at("y_win1", [P, S + SPARE], F32, RAW1 + S)]
-        for i, (e0, e1) in enumerate(pieces):
+        y_win = [at("y_win0", [P, S + SPARE], F32, RAW1 + 2 * S - SPARE), at("y_win1", [P, S + SPARE], F32, RAW1)]
+        for i, (e0, e1) in enumerate(halves):
             nc.scalar.copy(y_win[0][:, e0:e1], y0_acc[i][:])
         for i, (e0, e1) in enumerate(halves):
             nc.scalar.copy(y_win[1][:, e0:e1], y1_acc[i][:])
-        li = [sbuf("li%d" % b, [P, S], F32) for b in range(BLOCKS)]
+        li = [sbuf("li0", [P, S], F32, tag="g1b1"), sbuf("li1", [P, S], F32)]
         for b in range(BLOCKS):
             fused(li[b][:], y_win[b], inc_t, 0, S, sn_t[:], MULT)
         pairs = [li[b][:].rearrange("p (v d) -> p d v", d=2) for b in range(BLOCKS)]
 
         h_acc = [bank("h%d" % b, 3 + b, S) for b in range(BLOCKS)]
         g2 = [sbuf("g2_%d" % o, [P, N, PACK], BF16) for o in range(PASSES)]
-        interleave(g2[0][:], w2_raw[0], 0, N)
-        for b in range(BLOCKS):
-            interleave(g2[1][:, b * P : (b + 1) * P, :], w2_raw[1], b * P, P)
+        for o in range(PASSES):
+            interleave(g2[o][:], w2_raw[o], 0, N)
         dv_win0 = at("dv_win0", [P, 2 * S], F32, RAW2)
         nc.vector.tensor_tensor(dv_win0[:, 0:V], pairs[0][:, 0, :], pairs[0][:, 1, :], ADD)
         wq = quantize("q2_0", g2[0][:], N)
         for b in range(BLOCKS):
             open_wide(h_acc[b], wq, b * P)
-        for b in range(BLOCKS):
-            wq = quantize(
-                "q2_1%d" % b, g2[1][:, b * P : (b + 1) * P, :], P
-            )
-            close_wide(h_acc[b], wq, 0)
-        tail0 = at("tail0", [P, S], F32, RAW2 + 2 * S)
+        tail0 = sbuf("tail0", [P, S], F32)
         nc.vector.tensor_copy(tail0[:], dv_win0[:].indirect(tail_t[:]))
-        g3 = [sbuf("g3_0", [P, N, PACK], BF16), sbuf("g3_1", [P, N, PACK], BF16)]
-        own = [bank("own%d" % b, 5 + b, S) for b in range(BLOCKS)]
-        interleave(g3[0][:], w3_raw[0], 0, N)
-        wq = quantize("q3_0", g3[0][:], N)
+        wq = quantize("q2_1", g2[1][:], N)
         for b in range(BLOCKS):
-            open_wide(own[b], wq, b * P)
-        down0 = at("down0", [P, S], F32, RAW3[0])
+            close_wide(h_acc[b], wq, b * P)
+        down0 = at("down0", [P, S], F32, RAW2 + 2 * S)
         fused(down0[:], dv_win0, head_t, 0, S, tail0[:], SUB)
-        interleave(g3[1][:], w3_raw[1], 0, N)
-        wq = quantize("q3_1", g3[1][:], N)
-        for b in range(BLOCKS):
-            close_wide(own[b], wq, b * P)
-        h_win = [at("h_win%d" % b, [P, S], F32, RAW3[1] + b * S) for b in range(BLOCKS)]
-        for b in range(BLOCKS):
-            nc.scalar.copy(h_win[b][:], h_acc[b][:])
+        own = [bank("own%d" % b, 5 + b, S) for b in range(BLOCKS)]
+        for o in range(PASSES):
+            g3 = sbuf("g3_%d" % o, [P, N, PACK], BF16)
+            interleave(g3[:], w3_raw[o], 0, N)
+            wq = quantize("q3_%d" % o, g3[:], N)
+            for b in reversed(range(BLOCKS)):
+                (open_wide, close_wide)[o](own[b], wq, b * P)
+        h_win0 = at("h_win0", [P, S], F32, RAW3[1] - V)
+        dv1_turned = at("dv1_turned", [P, V], F32, RAW3[1] + V)
+        h_win = [h_win0, at("h_win1", [P, S], F32, RAW3[1] + S)]
+        nc.scalar.copy(h_win[0][:], h_acc[0][:])
+        add_turned("dv1", [pairs[1][:, d, :] for d in range(2)], 0, dv1_turned)
+        nc.scalar.copy(h_win[1][:], h_acc[1][:])
+        turn_back("dv1", dv1_turned, 1, dv_win1[:, 0:V])
+        own1 = sbuf("own1", [P, S], F32)
+        nc.scalar.copy(own1[:], own[1][:])
 
         sides = [sbuf("sides%d" % b, [P, 2 * V], F32) for b in range(BLOCKS)]
         cu_win = [at("cu_win0", [P, S + SPARE], F32, RAW2), cu_win1]
+        cu_turned = [sbuf("cu_turned0", [P, V], F32), sbuf("cu_turned1", [P, V], F32, tag="late")]
         for b in range(BLOCKS):
-            fused(sides[b][:, 0:V], h_win[b], tri_t, 0, V, sa_t[:], MULT)
+            fused(sides[b][:, 0:V], h_win[b], tri_t, 0, V, sa_t, MULT)
             fused(sides[b][:, V:], h_win[b], trj_t, 0, V, sb_t[:], MULT)
         for b in range(BLOCKS):
-            nc.vector.tensor_tensor(cu_win[b][:, 0:V], sides[b][:, 0:V], sides[b][:, V:], ADD)
-        dv1_turned = sbuf("dv1_turned", [P, V], F32)
-        add_turned("dv1", [pairs[1][:, d, :] for d in range(2)], 4, dv1_turned)
-        turn_back("dv1", dv1_turned, 7, dv_win1[:, 0:V])
+            add_turned("cu%d" % b, [sides[b][:, 0:V], sides[b][:, V:]], 7, cu_turned[b])
+            turn_back("cu%d" % b, cu_turned[b], (2, 1)[b], cu_win[b][:, 0:V])
+        plus1 = at("plus1", [P, S], F32, RAW3[1] - V)
+        fused(plus1[:], dv_win1, head_t, 0, S, own1[:], ADD)
         own0 = sbuf("own0", [P, S], F32)
         nc.scalar.copy(own0[:], own[0][:])
 
         up0 = sbuf("up0", [P, S], F32)
         fused(up0[:], cu_win[0], face_t, 0, S, sf_t, MULT)
 
-        sums = [bank("sum%d" % i, i, HALF) for i in range(2)]
+        sums = [bank("sum%d" % i, 3 + i, HALF) for i in range(2)]
 
         def add_term(term, first=False, last=False):
             for i, (e0, e1) in enumerate(halves):
@@ -282,7 +283,7 @@ def tile_picked_yhodge_tanh_p_kernel(
         for i in range(2):
             turned = sbuf("turned%d" % i, [P, HALF], F32)
             nc.scalar.activation(turned[:], sums[i][:], TANH)
-            back = bank("back%d" % i, 2 + i, HALF)
+            back = bank("back%d" % i, (7, 2)[i], HALF)
             for c in range(2):
                 nc.tensor.transpose(back[:, c * P : (c + 1) * P], turned[:, c * P : (c + 1) * P], ident[:])
             backs.append(back)
@@ -291,18 +292,25 @@ def tile_picked_yhodge_tanh_p_kernel(
             nc.scalar.copy(res[:], backs[i][:])
             nc.sync.dma_start(out[0:P, e0:e1], res[:])
 
+        neg1 = sbuf("neg1", [P, S], F32, tag="late")
+        fused(neg1[:], dv_win1, tail_t, 0, S, plus1[:], SUB)
         up1 = sbuf("up1", [P, S], F32)
-        rest1 = sbuf("rest1", [P, S], F32)
-        plus1 = sbuf("plus1", [P, S], F32)
-        for e0, e1 in halves:
+
+        def face1(i):
+            e0, e1 = pieces[i]
             fused(up1[:, e0:e1], cu_win[1], face_t, e0, e1, sf_t[:, e0:e1], MULT)
-        for e0, e1 in halves:
-            nc.vector.tensor_tensor(rest1[:, e0:e1], own[1][:, e0:e1], up1[:, e0:e1], ADD)
-        for e0, e1 in halves:
-            fused(plus1[:, e0:e1], dv_win1, head_t, e0, e1, rest1[:, e0:e1], ADD)
-        for e0, e1 in pieces:
-            neg = sbuf("neg%d" % e0, [P, e1 - e0], F32)
-            fused(neg[:], dv_win1, tail_t, e0, e1, plus1[:, e0:e1], SUB)
-            res = sbuf("res1%d" % e0, [P, e1 - e0], F32)
-            nc.scalar.activation(res[:], neg[:], TANH, scale=-1.0)
+
+        def finish1(i):
+            e0, e1 = pieces[i]
+            total = sbuf("total%d" % i, [P, e1 - e0], F32)
+            nc.vector.tensor_tensor(total[:], up1[:, e0:e1], neg1[:, e0:e1], SUB)
+            res = sbuf("res1%d" % i, [P, e1 - e0], F32)
+            nc.scalar.activation(res[:], total[:], TANH)
             nc.sync.dma_start(out[P : 2 * P, e0:e1], res[:])
+
+        face1(0)
+        face1(1)
+        finish1(0)
+        face1(2)
+        finish1(1)
+        finish1(2)

@@ -37,7 +37,7 @@ def tile_picked_yhodge_tanh_p_kernel(
         psum = ctx.enter_context(tc.psum_pool(name="psum", bufs=1))
 
         def sbuf(name, shape, dtype, tag=None):
-            return keep.tile(shape, dtype, name=name, tag=tag or name, align_bytes=64)
+            return keep.tile(shape, dtype, name=name, tag=tag or name, align_bytes=256)
 
         def bank(name, i, width):
             return psum.tile([P, width], F32, name=name, tag="bank%d" % i)
@@ -61,11 +61,12 @@ def tile_picked_yhodge_tanh_p_kernel(
             return t
 
         def at(name, shape, dtype, word):
-            return shared.tile(shape, dtype, name=name, offset=4 * word, align_bytes=64)
+            return shared.tile(shape, dtype, name=name, offset=4 * word, align_bytes=256 if word % 64 == 0 else 64)
 
         RAW1, RAW2 = 0, 4 * S
         W1_SLOT = {(0, 0): 0, (1, 0): 1, (0, 1): 2, (1, 1): 3}
         RAW3 = [8 * S, 10 * S]
+        TURNED = 12 * S + 192
 
         scale_all = sbuf("scale_all", [P, T], U8)
         nc.gpsimd.memset(scale_all[:].bitcast(I32), 0)
@@ -207,13 +208,13 @@ def tile_picked_yhodge_tanh_p_kernel(
             nc.scalar.copy(y_win[0][:, e0:e1], y0_acc[i][:])
         for i, (e0, e1) in enumerate(halves):
             nc.scalar.copy(y_win[1][:, e0:e1], y1_acc[i][:])
-        li = [sbuf("li0", [P, S], F32, tag="g1b1"), sbuf("li1", [P, S], F32)]
+        li = [at("li0", [P, S], F32, RAW1 + 3 * S), sbuf("li1", [P, S], F32)]
         for b in range(BLOCKS):
             fused(li[b][:], y_win[b], inc_t, 0, S, sn_t[:], MULT)
         pairs = [li[b][:].rearrange("p (v d) -> p d v", d=2) for b in range(BLOCKS)]
 
         h_acc = [bank("h%d" % b, 3 + b, S) for b in range(BLOCKS)]
-        g2 = [sbuf("g2_%d" % o, [P, N, PACK], BF16) for o in range(PASSES)]
+        g2 = [sbuf("g2_0", [P, N, PACK], BF16, tag="q1_11_codes"), sbuf("g2_1", [P, N, PACK], BF16)]
         for o in range(PASSES):
             interleave(g2[o][:], w2_raw[o], 0, N)
         dv_win0 = at("dv_win0", [P, 2 * S], F32, RAW2)
@@ -260,9 +261,10 @@ def tile_picked_yhodge_tanh_p_kernel(
         nc.scalar.copy(own0[:], own[0][:])
 
         up0 = sbuf("up0", [P, S], F32)
-        fused(up0[:], cu_win[0], face_t, 0, S, sf_t, MULT)
+        for e0, e1 in halves:
+            fused(up0[:, e0:e1], cu_win[0], face_t, e0, e1, sf_t[:, e0:e1], MULT)
 
-        sums = [bank("sum%d" % i, 3 + i, HALF) for i in range(2)]
+        sums = [bank("sum%d" % i, (7, 4)[i], HALF) for i in range(2)]
 
         def add_term(term, first=False, last=False):
             for i, (e0, e1) in enumerate(halves):
@@ -281,9 +283,9 @@ def tile_picked_yhodge_tanh_p_kernel(
         add_term(up0, last=True)
         backs = []
         for i in range(2):
-            turned = sbuf("turned%d" % i, [P, HALF], F32)
+            turned = at("turned%d" % i, [P, HALF], F32, (TURNED + 3 * P, TURNED)[i])
             nc.scalar.activation(turned[:], sums[i][:], TANH)
-            back = bank("back%d" % i, (7, 2)[i], HALF)
+            back = bank("back%d" % i, (3, 2)[i], HALF)
             for c in range(2):
                 nc.tensor.transpose(back[:, c * P : (c + 1) * P], turned[:, c * P : (c + 1) * P], ident[:])
             backs.append(back)
@@ -304,7 +306,7 @@ def tile_picked_yhodge_tanh_p_kernel(
             e0, e1 = pieces[i]
             total = sbuf("total%d" % i, [P, e1 - e0], F32)
             nc.vector.tensor_tensor(total[:], up1[:, e0:e1], neg1[:, e0:e1], SUB)
-            res = sbuf("res1%d" % i, [P, e1 - e0], F32)
+            res = at("res1%d" % i, [P, e1 - e0], F32, TURNED - 192 + e0)
             nc.scalar.activation(res[:], total[:], TANH)
             nc.sync.dma_start(out[P : 2 * P, e0:e1], res[:])
 

@@ -213,20 +213,23 @@ def tile_picked_yhodge_tanh_p_kernel(
             fused(li[b][:], y_win[b], inc_t, 0, S, sn_t[:], MULT)
         pairs = [li[b][:].rearrange("p (v d) -> p d v", d=2) for b in range(BLOCKS)]
 
-        h_acc = [bank("h%d" % b, 3 + b, S) for b in range(BLOCKS)]
+        h0_acc = [bank("h0%d" % i, (3, 7)[i], HALF) for i in range(2)]
+        h1_acc = bank("h1", 4, S)
         g2 = [sbuf("g2_0", [P, N, PACK], BF16, tag="q1_11_codes"), sbuf("g2_1", [P, N, PACK], BF16)]
         for o in range(PASSES):
             interleave(g2[o][:], w2_raw[o], 0, N)
         dv_win0 = at("dv_win0", [P, 2 * S], F32, RAW2)
         nc.vector.tensor_tensor(dv_win0[:, 0:V], pairs[0][:, 0, :], pairs[0][:, 1, :], ADD)
         wq = quantize("q2_0", g2[0][:], N)
-        for b in range(BLOCKS):
-            open_wide(h_acc[b], wq, b * P)
+        for i, (e0, e1) in enumerate(halves):
+            mx_pass(h0_acc[i][:], wq, 0, 0, e0, e1, True, False)
+        open_wide(h1_acc, wq, P)
         tail0 = sbuf("tail0", [P, S], F32)
         nc.vector.tensor_copy(tail0[:], dv_win0[:].indirect(tail_t[:]))
         wq = quantize("q2_1", g2[1][:], N)
-        for b in range(BLOCKS):
-            close_wide(h_acc[b], wq, b * P)
+        for i, (e0, e1) in enumerate(halves):
+            mx_pass(h0_acc[i][:], wq, 0, 1, e0, e1, False, True)
+        close_wide(h1_acc, wq, P)
         down0 = at("down0", [P, S], F32, RAW2 + 2 * S)
         fused(down0[:], dv_win0, head_t, 0, S, tail0[:], SUB)
         own = [bank("own%d" % b, 5 + b, S) for b in range(BLOCKS)]
@@ -239,22 +242,34 @@ def tile_picked_yhodge_tanh_p_kernel(
         h_win0 = at("h_win0", [P, S], F32, RAW3[1] - V)
         dv1_turned = at("dv1_turned", [P, V], F32, RAW3[1] + V)
         h_win = [h_win0, at("h_win1", [P, S], F32, RAW3[1] + S)]
-        nc.scalar.copy(h_win[0][:], h_acc[0][:])
+        for i, (e0, e1) in enumerate(halves):
+            nc.scalar.copy(h_win[0][:, e0:e1], h0_acc[i][:])
         add_turned("dv1", [pairs[1][:, d, :] for d in range(2)], 0, dv1_turned)
-        nc.scalar.copy(h_win[1][:], h_acc[1][:])
+        nc.scalar.copy(h_win[1][:], h1_acc[:])
         turn_back("dv1", dv1_turned, 1, dv_win1[:, 0:V])
         own1 = sbuf("own1", [P, S], F32)
         nc.scalar.copy(own1[:], own[1][:])
 
         sides = [sbuf("sides%d" % b, [P, 2 * V], F32) for b in range(BLOCKS)]
         cu_win = [at("cu_win0", [P, S + SPARE], F32, RAW2), cu_win1]
-        cu_turned = [sbuf("cu_turned0", [P, V], F32), sbuf("cu_turned1", [P, V], F32, tag="late")]
+        cu_turned = [sbuf("cu_turned0", [P, V], F32, tag="own0"), sbuf("cu_turned1", [P, V], F32, tag="late")]
         for b in range(BLOCKS):
             fused(sides[b][:, 0:V], h_win[b], tri_t, 0, V, sa_t, MULT)
             fused(sides[b][:, V:], h_win[b], trj_t, 0, V, sb_t[:], MULT)
-        for b in range(BLOCKS):
-            add_turned("cu%d" % b, [sides[b][:, 0:V], sides[b][:, V:]], 7, cu_turned[b])
-            turn_back("cu%d" % b, cu_turned[b], (2, 1)[b], cu_win[b][:, 0:V])
+        for c in range(2):
+            acc = bank("cu0_sum%d" % c, (7, 0)[c], P)
+            for d in range(2):
+                nc.tensor.matmul(
+                    acc[:], sides[0][:, d * V + c * P : d * V + (c + 1) * P], ident[:],
+                    start=d == 0, stop=d == 1, is_transpose=True,
+                )
+            nc.scalar.copy(cu_turned[0][:, c * P : (c + 1) * P], acc[:])
+        for c in range(2):
+            back = bank("cu0_back%d" % c, (2, 3)[c], P)
+            nc.tensor.transpose(back[:], cu_turned[0][:, c * P : (c + 1) * P], ident[:])
+            nc.scalar.copy(cu_win[0][:, c * P : (c + 1) * P], back[:])
+        add_turned("cu1", [sides[1][:, 0:V], sides[1][:, V:]], 0, cu_turned[1])
+        turn_back("cu1", cu_turned[1], 1, cu_win[1][:, 0:V])
         plus1 = at("plus1", [P, S], F32, RAW3[1] - V)
         fused(plus1[:], dv_win1, head_t, 0, S, own1[:], ADD)
         own0 = sbuf("own0", [P, S], F32)
@@ -264,7 +279,8 @@ def tile_picked_yhodge_tanh_p_kernel(
         for e0, e1 in halves:
             fused(up0[:, e0:e1], cu_win[0], face_t, e0, e1, sf_t[:, e0:e1], MULT)
 
-        sums = [bank("sum%d" % i, (7, 4)[i], HALF) for i in range(2)]
+
+        sums = [bank("sum%d" % i, (0, 4)[i], HALF) for i in range(2)]
 
         def add_term(term, first=False, last=False):
             for i, (e0, e1) in enumerate(halves):

@@ -22,9 +22,9 @@ U16 = mybir.dt.uint16
 U8 = mybir.dt.uint8
 FP8X4 = mybir.dt.float8_e4m3fn_x4
 ADD = mybir.AluOpType.add
-SUB = mybir.AluOpType.subtract
 MULT = mybir.AluOpType.mult
 TANH = mybir.ActivationFunctionType.Tanh
+COPY = mybir.ActivationFunctionType.Copy
 
 
 def tile_picked_yhodge_tanh_p_kernel(
@@ -39,6 +39,27 @@ def tile_picked_yhodge_tanh_p_kernel(
         def sbuf(name, shape, dtype, tag=None):
             return keep.tile(shape, dtype, name=name, tag=tag or name, align_bytes=256)
 
+        def at(name, shape, dtype, word):
+            return shared.tile(shape, dtype, name=name, offset=4 * word, align_bytes=256)
+
+        def place(name, shape, dtype, word):
+            return sbuf(name, shape, dtype) if word is None else at(name, shape, dtype, word)
+
+        RAW1 = 0
+        RAW2 = [2 * S, 4 * S]
+        LI1 = RAW2[1] + S + 64
+        CODES2 = LI1 + S
+        RAW3_FIRST = CODES2 + S
+        RAW3 = RAW3_FIRST + 3 * S
+        UP0 = RAW3 - S + 64
+        CU1 = RAW3 + 64
+        HEAD0 = RAW3 + 384
+        TAIL1 = HEAD0 + S
+        HEAD1 = TAIL1 + S
+        CODES3 = HEAD1 + HALF - 64
+        OWN0 = CODES3 + N
+        TURNED = OWN0 + S + 192
+
         def bank(name, i, width):
             return psum.tile([P, width], F32, name=name, tag="bank%d" % i)
 
@@ -47,35 +68,27 @@ def tile_picked_yhodge_tanh_p_kernel(
             nc.sync.dma_start(t[:], src)
             return t
 
-
         def load_words(o):
             t = sbuf("x_all%d" % o, [P, T], U32)
             nc.sync.dma_start(t[:].bitcast(I32), x_words[o].rearrange("p c r -> p (c r)").bitcast(I32))
-            return t[:]
+            return t
 
-        def load_weight(name, w, o, c0=0, width=N, t=None):
-            if t is None:
-                t = sbuf("%s_raw%d" % (name, o), [P, PACK, width], F32)
+        def load_weight(name, w, o, c0=0, width=N, word=None):
+            t = place(name, [P, PACK, width], F32, word)
             rows = w[o * K_PASS : (o + 1) * K_PASS, c0 : c0 + width]
             nc.sync.dma_start(t[:], rows.rearrange("(p t) c -> p t c", t=PACK))
             return t
 
-        def at(name, shape, dtype, word):
-            return shared.tile(shape, dtype, name=name, offset=4 * word, align_bytes=256 if word % 64 == 0 else 64)
-
-        RAW1, RAW2 = 0, 4 * S
-        W1_SLOT = {(0, 0): 0, (1, 0): 1, (0, 1): 2, (1, 1): 3}
-        RAW3 = [8 * S, 10 * S]
-        TURNED = 12 * S + 192
+        def window(name, used, width):
+            t = sbuf(name, [P, width], F32)
+            nc.vector.memset(t[:, used:], 0.0)
+            return t
 
         scale_all = sbuf("scale_all", [P, T], U8)
         nc.gpsimd.memset(scale_all[:].bitcast(I32), 0)
         zeros = sbuf("zeros", [P, SPARE], F32)
         nc.vector.memset(zeros[:], 0.0)
-        dv_win1 = sbuf("dv_win1", [P, 2 * S], F32)
-        sf_t = dv_win1[:, V : V + S]
-        sa_t = dv_win1[:, V + S :]
-        cu_win1 = sbuf("cu_win1", [P, V + SPARE], F32)
+        y_win0 = sbuf("y_win0", [P, S + SPARE], F32)
 
         x_all = [load_words(0)]
         offs_t = load("offs_t", offs, U16)
@@ -84,14 +97,16 @@ def tile_picked_yhodge_tanh_p_kernel(
                 scale_all[32 * q : 32 * q + PASSES * SCALE_ROWS, :].bitcast(I32),
                 x_scales[:, SCALE_ROWS * q : SCALE_ROWS * (q + 1), :].bitcast(I32),
             )
-        nc.scalar.activation(cu_win1[:, V:], zeros[:], TANH)
+        nc.scalar.activation(y_win0[:, S:], zeros[:], TANH)
         ident = sbuf("ident", [P, P], F32)
         make_identity(nc, ident[:])
+        y_win = [y_win0, window("y_win1", S, S + SPARE)]
+
         w1_raw = {}
 
         def load_w1(o, b):
-            t = at("w1_raw%d%d" % (o, b), [P, PACK, P], F32, RAW1 + W1_SLOT[o, b] * S)
-            w1_raw[o, b] = load_weight("w1", w1, o, b * P, P, t=t)
+            word = RAW1 + o * S if b == 0 else None
+            w1_raw[o, b] = load_weight("w1_raw%d%d" % (o, b), w1, o, b * P, P, word)
 
         load_w1(0, 0)
         x_all.append(load_words(1))
@@ -100,235 +115,228 @@ def tile_picked_yhodge_tanh_p_kernel(
         load_w1(1, 1)
         inc_t = load("inc_t", inc, U16)
         sn_t = load("sn_t", sn, F32)
-        w2_raw = [load_weight("w2", w2, o, t=at("w2_raw%d" % o, [P, PACK, N], F32, RAW2 + o * 2 * S)) for o in range(PASSES)]
+        w2_raw = [load_weight("w2_raw%d" % o, w2, o, word=RAW2[o]) for o in range(PASSES)]
         tail_t = load("tail_t", tail, U16)
         head_t = load("head_t", head, U16)
-        w3_raw = [load_weight("w3", w3, o, t=at("w3_raw%d" % o, [P, PACK, N], F32, RAW3[o])) for o in range(PASSES)]
         tri_t = load("tri_t", tri, U16)
         trj_t = load("trj_t", trj, U16)
-        nc.sync.dma_start(sa_t, sa)
+        sa_t = load("sa_t", sa, F32)
         sb_t = load("sb_t", sb, F32)
+        w3_raw = [load_weight("w3_raw%d" % o, w3, o, word=(RAW3_FIRST, RAW3)[o]) for o in range(PASSES)]
         face_t = load("face_t", face, U16)
-        nc.sync.dma_start(sf_t, sf)
+        sf_t = load("sf_t", sf, F32)
 
         def cols(lst, e0, e1):
             return lst[:, e0 // 16 : e1 // 16]
 
         halves = [(0, HALF), (HALF, S)]
-        x_pick = [sbuf("x_pick0", [P, S], U32), sbuf("x_pick1", [P, S], U32)]
-
-        def picked(o, e0, e1):
-            return x_pick[o][:, e0:e1]
-
+        x_pick = [sbuf("x_pick%d" % o, [P, S], U32) for o in range(PASSES)]
         scale_pick = sbuf("scale_pick", [P, S], U8)
-        nc.vector.tensor_copy(x_pick[0][:], x_all[0].indirect(offs_t[:]))
+        nc.vector.tensor_copy(x_pick[0][:], x_all[0][:].indirect(offs_t[:]))
         nc.vector.tensor_copy(scale_pick[:], scale_all[:].indirect(offs_t[:]))
 
-
-        def interleave(dst, raw, c0, width, copy=nc.scalar.copy):
+        def interleave(name, raw, width, copy, word=None):
+            grouped = place(name, [P, width, PACK], BF16, word)
             copy(
-                dst.rearrange("p (c i) t -> p c t i", i=4),
-                raw[:, :, c0 : c0 + width].rearrange("p t (c i) -> p c t i", i=4),
+                grouped[:].rearrange("p (c i) t -> p c t i", i=4),
+                raw[:].rearrange("p t (c i) -> p c t i", i=4),
             )
+            return grouped
 
-        def quantize(name, grouped, width, codes=None):
-            if codes is None:
-                codes = sbuf(name + "_codes", [P, width], U32)[:]
-            scales = sbuf(name + "_scales", [P, width], U8)
+        def quantize(name, grouped, width, words=(None, None)):
+            codes = place(name + "_codes", [P, width], U32, words[0])
+            scales = place(name + "_scales", [P, width], U8, words[1])
             nc.vector.quantize_mx(
-                out=codes.bitcast(FP8X4), scales=scales[:], in_=grouped.rearrange("p c t -> p (c t)")
+                out=codes[:].bitcast(FP8X4), scales=scales[:], in_=grouped.rearrange("p c t -> p (c t)")
             )
             return codes, scales
 
-        def mx_pass(acc, wq, c0, o, e0, e1, start, stop):
+        def mx_pass(acc, wq, c0, o, e0, e1):
             codes, scales = wq
             nc.tensor.matmul_mx(
                 out=acc,
                 lhsT=codes[:, c0 : c0 + P].bitcast(FP8X4),
                 lhsT_scale=scales[:, c0 : c0 + P],
-                rhs=picked(o, e0, e1).bitcast(FP8X4),
+                rhs=x_pick[o][:, e0:e1].bitcast(FP8X4),
                 rhs_scale=scale_pick[SCALE_ROWS * o :, e0:e1],
-                start=start,
-                stop=stop,
+                start=o == 0,
+                stop=o == PASSES - 1,
             )
 
-        def open_wide(acc, wq, c0):
-            mx_pass(acc[:], wq, c0, 0, 0, S, True, False)
+        def signed(dst, win, lst, e0, e1, sign):
+            nc.vector.tensor_tensor(dst, win[:].indirect(cols(lst, e0, e1)), sign, MULT)
 
-        def close_wide(acc, wq, c0):
-            mx_pass(acc[:], wq, c0, 1, 0, S, False, True)
+        def fetch(name, win, lst, factor, word=None):
+            t = place(name, [P, S], F32, word)
+            nc.scalar.activation(t[:], win[:].indirect(lst[:]), COPY, scale=factor)
+            return t
 
-        def fused(dst, window, lst, e0, e1, other, op):
-            nc.vector.tensor_tensor(dst, window[:].indirect(cols(lst, e0, e1)), other, op)
+        def add_turned(acc, term, first=False, last=False):
+            for c in range(2):
+                nc.tensor.matmul(
+                    acc[:, c * P : (c + 1) * P],
+                    term[:, c * P : (c + 1) * P],
+                    ident[:],
+                    start=first and c == 0,
+                    stop=last and c == 1,
+                    is_transpose=True,
+                )
 
-        def add_turned(name, terms, sum_bank, turned):
-            acc = bank(name + "_sum", sum_bank, V)
-            for d in range(2):
-                for c in range(2):
-                    nc.tensor.matmul(
-                        acc[:, c * P : (c + 1) * P],
-                        terms[d][:, c * P : (c + 1) * P],
-                        ident[:],
-                        start=d == 0 and c == 0,
-                        stop=d == 1 and c == 1,
-                        is_transpose=True,
-                    )
-            nc.scalar.copy(turned[:], acc[:])
-
-        def turn_back(name, turned, back_bank, dst):
-            back = bank(name + "_back", back_bank, V)
+        def turn_back(name, turned, i):
+            back = bank(name, i, HALF)
             for c in range(2):
                 nc.tensor.transpose(back[:, c * P : (c + 1) * P], turned[:, c * P : (c + 1) * P], ident[:])
-            nc.scalar.copy(dst, back[:])
+            return back
 
-        pieces = [(0, HALF), (HALF, HALF + P), (HALF + P, S)]
-        y0_acc = [bank("y0%d" % i, i, HALF) for i in range(2)]
-        y1_acc = [bank("y1%d" % i, (2, 5)[i], HALF) for i in range(2)]
-        g1a = sbuf("g1a", [P, PASSES * P, PACK], BF16)
-        g1b = [sbuf("g1b%d" % o, [P, P, PACK], BF16) for o in range(PASSES)]
-        for o in range(PASSES):
-            interleave(g1a[:, o * P : (o + 1) * P, :], w1_raw[o, 0], 0, P)
-        interleave(g1b[0][:], w1_raw[0, 1], 0, P)
-        codes_a = sbuf("codes_a", [P, PASSES * P], U32)
-        wq = quantize("q1_00", g1a[:, 0:P, :], P, codes=codes_a[:, 0:P])
-        for i, (e0, e1) in enumerate(halves):
-            mx_pass(y0_acc[i][:], wq, 0, 0, e0, e1, True, False)
-        nc.vector.tensor_copy(x_pick[1][:], x_all[1].indirect(offs_t[:]))
-        wq = quantize("q1_01", g1a[:, P:, :], P, codes=codes_a[:, P:])
-        for i, (e0, e1) in enumerate(halves):
-            mx_pass(y0_acc[i][:], wq, 0, 1, e0, e1, False, True)
-        for o in range(PASSES):
-            if o == 1:
-                interleave(g1b[1][:], w1_raw[1, 1], 0, P, nc.vector.tensor_copy)
-            wq = quantize("q1_1%d" % o, g1b[o][:], P)
+        on_scalar, on_vector = nc.scalar.copy, nc.vector.tensor_copy
+
+        y_acc = [[bank("y%d%d" % (b, i), 2 * b + i, HALF) for i in range(2)] for b in range(BLOCKS)]
+        g1 = {}
+        for o, b in ((0, 0), (1, 0), (0, 1)):
+            g1[o, b] = interleave("g1_%d%d" % (o, b), w1_raw[o, b], P, on_scalar)
+
+        def y_passes(o, b):
+            wq = quantize("q1_%d%d" % (o, b), g1[o, b][:], P)
             for i, (e0, e1) in enumerate(halves):
-                mx_pass(y1_acc[i][:], wq, 0, o, e0, e1, o == 0, o == 1)
-        y_win = [at("y_win0", [P, S + SPARE], F32, RAW1 + 2 * S - SPARE), at("y_win1", [P, S + SPARE], F32, RAW1)]
-        for i, (e0, e1) in enumerate(halves):
-            nc.scalar.copy(y_win[0][:, e0:e1], y0_acc[i][:])
-        for i, (e0, e1) in enumerate(halves):
-            nc.scalar.copy(y_win[1][:, e0:e1], y1_acc[i][:])
-        li = [at("li0", [P, S], F32, RAW1 + 3 * S), sbuf("li1", [P, S], F32)]
-        for b in range(BLOCKS):
-            fused(li[b][:], y_win[b], inc_t, 0, S, sn_t[:], MULT)
-        pairs = [li[b][:].rearrange("p (v d) -> p d v", d=2) for b in range(BLOCKS)]
+                mx_pass(y_acc[b][i][:], wq, 0, o, e0, e1)
 
-        h0_acc = [bank("h0%d" % i, (3, 7)[i], HALF) for i in range(2)]
-        h1_acc = bank("h1", 4, S)
-        g2 = [sbuf("g2_0", [P, N, PACK], BF16, tag="q1_11_codes"), sbuf("g2_1", [P, N, PACK], BF16)]
-        for o in range(PASSES):
-            interleave(g2[o][:], w2_raw[o], 0, N)
-        dv_win0 = at("dv_win0", [P, 2 * S], F32, RAW2)
-        nc.vector.tensor_tensor(dv_win0[:, 0:V], pairs[0][:, 0, :], pairs[0][:, 1, :], ADD)
-        wq = quantize("q2_0", g2[0][:], N)
+        y_passes(0, 0)
+        nc.vector.tensor_copy(x_pick[1][:], x_all[1][:].indirect(offs_t[:]))
+        y_passes(1, 0)
+        g1[1, 1] = interleave("g1_11", w1_raw[1, 1], P, on_vector)
+        y_passes(0, 1)
+        y_passes(1, 1)
+        for b in range(BLOCKS):
+            for i, (e0, e1) in enumerate(halves):
+                nc.scalar.copy(y_win[b][:, e0:e1], y_acc[b][i][:])
+
+        def incidence(b, word=None):
+            li = place("li%d" % b, [P, S], F32, word)
+            signed(li[:], y_win[b], inc_t, 0, S, sn_t[:])
+            return li
+
+        def node_sum(b, li):
+            win = at("dv_win%d" % b, [P, S + SPARE], F32, (RAW1, RAW2[1])[b])
+            pairs = li[:].rearrange("p (v d) -> p d v", d=2)
+            nc.vector.tensor_tensor(win[:, 0:V], pairs[:, 0, :], pairs[:, 1, :], ADD)
+            return win
+
+        g2 = sbuf("g2", [P, BLOCKS, PASSES * P, PACK], BF16)
+
+        def interleave_w2(o, copy, b0=0, b1=BLOCKS):
+            copy(
+                g2[:, b0:b1, o * P : (o + 1) * P, :].rearrange("p b (c i) t -> p b c t i", i=4),
+                w2_raw[o][:, :, b0 * P : b1 * P].rearrange("p t (b c i) -> p b c t i", b=b1 - b0, i=4),
+            )
+
+        h0_acc = [bank("h0%d" % i, (4, 0)[i], HALF) for i in range(2)]
+        h1_acc = bank("h1", 5, S)
+        interleave_w2(0, on_scalar)
+        li0 = incidence(0)
+        dv_win = [node_sum(0, li0)]
+        for b in range(BLOCKS):
+            interleave_w2(1, on_vector, b, b + 1)
+        wq = quantize("q2_0", g2[:, 0], N, (CODES2, None))
         for i, (e0, e1) in enumerate(halves):
-            mx_pass(h0_acc[i][:], wq, 0, 0, e0, e1, True, False)
-        open_wide(h1_acc, wq, P)
-        tail0 = sbuf("tail0", [P, S], F32)
-        nc.vector.tensor_copy(tail0[:], dv_win0[:].indirect(tail_t[:]))
-        wq = quantize("q2_1", g2[1][:], N)
-        for i, (e0, e1) in enumerate(halves):
-            mx_pass(h0_acc[i][:], wq, 0, 1, e0, e1, False, True)
-        close_wide(h1_acc, wq, P)
-        down0 = at("down0", [P, S], F32, RAW2 + 2 * S)
-        fused(down0[:], dv_win0, head_t, 0, S, tail0[:], SUB)
-        own = [bank("own%d" % b, 5 + b, S) for b in range(BLOCKS)]
+            for o in range(PASSES):
+                mx_pass(h0_acc[i][:], wq, o * P, o, e0, e1)
+        li1 = incidence(1, LI1)
+        wq = quantize("q2_1", g2[:, 1], N)
         for o in range(PASSES):
-            g3 = sbuf("g3_%d" % o, [P, N, PACK], BF16)
-            interleave(g3[:], w3_raw[o], 0, N)
-            wq = quantize("q3_%d" % o, g3[:], N)
-            for b in reversed(range(BLOCKS)):
-                (open_wide, close_wide)[o](own[b], wq, b * P)
-        h_win0 = at("h_win0", [P, S], F32, RAW3[1] - V)
-        dv1_turned = at("dv1_turned", [P, V], F32, RAW3[1] + V)
-        h_win = [h_win0, at("h_win1", [P, S], F32, RAW3[1] + S)]
+            mx_pass(h1_acc[:], wq, o * P, o, 0, S)
+        dv_win.append(node_sum(1, li1))
+
+        own_acc = [bank("own%d" % b, 6 + b, S) for b in range(BLOCKS)]
+        sum0 = [bank("sum0%d" % i, (4, 0)[i], HALF) for i in range(2)]
+        h_win = [sbuf("h_win0", [P, S], F32), at("h_win1", [P, S], F32, RAW3_FIRST)]
+        sides = [sbuf("sides%d" % b, [P, 2 * V], F32) for b in range(BLOCKS)]
+        cu_win = [at("cu_win%d" % b, [P, V + SPARE], F32, (RAW3_FIRST + S, CU1)[b]) for b in range(BLOCKS)]
+        up = [at("up0", [P, S], F32, UP0), sbuf("up1", [P, S], F32)]
+
+        def curl_term(b, d):
+            signed(sides[b][:, d * V : (d + 1) * V], h_win[b], (tri_t, trj_t)[d], 0, V, (sa_t, sb_t)[d][:])
+
+        def curl_sum(b):
+            nc.vector.tensor_tensor(cu_win[b][:, 0:V], sides[b][:, 0:V], sides[b][:, V:], ADD)
+
+        def face_term(b, e0, e1):
+            signed(up[b][:, e0:e1], cu_win[b], face_t, e0, e1, sf_t[:, e0:e1])
+
+        def own_passes(o, grouped):
+            wq = quantize("q3_%d" % o, grouped[:], N, ((None, CODES3)[o], None))
+            for b in range(BLOCKS):
+                mx_pass(own_acc[b][:], wq, b * P, o, 0, S)
+
+        def fetch_head(b, i, word):
+            t = place("head%d%d" % (b, i), [P, HALF], F32, word)
+            nc.scalar.activation(t[:], dv_win[b][:].indirect(cols(head_t, *halves[i])), COPY)
+            return t
+
+        tail0 = fetch("tail0", dv_win[0], tail_t, -1.0)
+        head0 = [fetch_head(0, 0, None)]
         for i, (e0, e1) in enumerate(halves):
             nc.scalar.copy(h_win[0][:, e0:e1], h0_acc[i][:])
-        add_turned("dv1", [pairs[1][:, d, :] for d in range(2)], 0, dv1_turned)
+        for i, (e0, e1) in enumerate(halves):
+            add_turned(sum0[i], tail0[:, e0:e1], first=True)
+        g3_0 = interleave("g3_0", w3_raw[0], N, on_scalar, CODES2)
+        g3_1 = interleave("g3_1", w3_raw[1], N, on_scalar)
         nc.scalar.copy(h_win[1][:], h1_acc[:])
-        turn_back("dv1", dv1_turned, 1, dv_win1[:, 0:V])
-        own1 = sbuf("own1", [P, S], F32)
-        nc.scalar.copy(own1[:], own[1][:])
-
-        sides = [sbuf("sides%d" % b, [P, 2 * V], F32) for b in range(BLOCKS)]
-        cu_win = [at("cu_win0", [P, S + SPARE], F32, RAW2), cu_win1]
-        cu_turned = [sbuf("cu_turned0", [P, V], F32, tag="own0"), sbuf("cu_turned1", [P, V], F32, tag="late")]
-        for b in range(BLOCKS):
-            fused(sides[b][:, 0:V], h_win[b], tri_t, 0, V, sa_t, MULT)
-            fused(sides[b][:, V:], h_win[b], trj_t, 0, V, sb_t[:], MULT)
-        for c in range(2):
-            acc = bank("cu0_sum%d" % c, (7, 0)[c], P)
-            for d in range(2):
-                nc.tensor.matmul(
-                    acc[:], sides[0][:, d * V + c * P : d * V + (c + 1) * P], ident[:],
-                    start=d == 0, stop=d == 1, is_transpose=True,
-                )
-            nc.scalar.copy(cu_turned[0][:, c * P : (c + 1) * P], acc[:])
-        for c in range(2):
-            back = bank("cu0_back%d" % c, (2, 3)[c], P)
-            nc.tensor.transpose(back[:], cu_turned[0][:, c * P : (c + 1) * P], ident[:])
-            nc.scalar.copy(cu_win[0][:, c * P : (c + 1) * P], back[:])
-        add_turned("cu1", [sides[1][:, 0:V], sides[1][:, V:]], 0, cu_turned[1])
-        turn_back("cu1", cu_turned[1], 1, cu_win[1][:, 0:V])
-        plus1 = at("plus1", [P, S], F32, RAW3[1] - V)
-        fused(plus1[:], dv_win1, head_t, 0, S, own1[:], ADD)
-        own0 = sbuf("own0", [P, S], F32)
-        nc.scalar.copy(own0[:], own[0][:])
-
-        up0 = sbuf("up0", [P, S], F32)
-        for e0, e1 in halves:
-            fused(up0[:, e0:e1], cu_win[0], face_t, e0, e1, sf_t[:, e0:e1], MULT)
-
-
-        sums = [bank("sum%d" % i, (0, 4)[i], HALF) for i in range(2)]
-
-        def add_term(term, first=False, last=False):
-            for i, (e0, e1) in enumerate(halves):
-                for c in range(2):
-                    nc.tensor.matmul(
-                        sums[i][:, c * P : (c + 1) * P],
-                        term[:, e0 + c * P : e0 + (c + 1) * P],
-                        ident[:],
-                        start=first and c == 0,
-                        stop=last and c == 1,
-                        is_transpose=True,
-                    )
-
-        add_term(down0, first=True)
-        add_term(own0)
-        add_term(up0, last=True)
+        curl_term(0, 0)
+        curl_term(0, 1)
+        own_passes(0, g3_0)
+        curl_sum(0)
+        own_passes(1, g3_1)
+        face_term(0, 0, HALF)
+        curl_term(1, 0)
+        curl_term(1, 1)
+        face_term(0, HALF, S)
+        curl_sum(1)
+        head0.append(fetch_head(0, 1, HEAD0))
+        tail1 = fetch("tail1", dv_win[1], tail_t, -1.0, TAIL1)
+        own0 = at("own0_sb", [P, S], F32, OWN0)
+        nc.scalar.copy(own0[:], own_acc[0][:])
+        head1 = [fetch_head(1, 0, HEAD1)]
+        add_turned(sum0[0], up[0][:, 0:HALF])
+        for i in range(2):
+            add_turned(sum0[i], head0[i])
+        add_turned(sum0[1], up[0][:, HALF:])
+        for i, (e0, e1) in enumerate(halves):
+            add_turned(sum0[i], own0[:, e0:e1], last=True)
         backs = []
         for i in range(2):
-            turned = at("turned%d" % i, [P, HALF], F32, (TURNED + 3 * P, TURNED)[i])
-            nc.scalar.activation(turned[:], sums[i][:], TANH)
-            back = bank("back%d" % i, (3, 2)[i], HALF)
-            for c in range(2):
-                nc.tensor.transpose(back[:, c * P : (c + 1) * P], turned[:, c * P : (c + 1) * P], ident[:])
-            backs.append(back)
-        for i, (e0, e1) in enumerate(halves):
+            turned = at("turned0%d" % i, [P, HALF], F32, (TURNED + 3 * P, TURNED)[i])
+            nc.scalar.activation(turned[:], sum0[i][:], TANH)
+            backs.append(turn_back("back0%d" % i, turned, 1 + i))
+
+        def store0(i, copy):
+            e0, e1 = halves[i]
             res = sbuf("res0%d" % i, [P, HALF], F32)
-            nc.scalar.copy(res[:], backs[i][:])
+            copy(res[:], backs[i][:])
             nc.sync.dma_start(out[0:P, e0:e1], res[:])
 
-        neg1 = sbuf("neg1", [P, S], F32, tag="late")
-        fused(neg1[:], dv_win1, tail_t, 0, S, plus1[:], SUB)
-        up1 = sbuf("up1", [P, S], F32)
+        part1 = sbuf("part1", [P, S], F32)
+        rest1 = sbuf("rest1", [P, S], F32)
+        total1 = sbuf("total1", [P, S], F32)
 
-        def face1(i):
-            e0, e1 = pieces[i]
-            fused(up1[:, e0:e1], cu_win[1], face_t, e0, e1, sf_t[:, e0:e1], MULT)
+        def add_head1(i):
+            e0, e1 = halves[i]
+            nc.vector.tensor_tensor(rest1[:, e0:e1], part1[:, e0:e1], head1[i][:], ADD)
 
-        def finish1(i):
-            e0, e1 = pieces[i]
-            total = sbuf("total%d" % i, [P, e1 - e0], F32)
-            nc.vector.tensor_tensor(total[:], up1[:, e0:e1], neg1[:, e0:e1], SUB)
-            res = at("res1%d" % i, [P, e1 - e0], F32, TURNED - 192 + e0)
-            nc.scalar.activation(res[:], total[:], TANH)
+        def finish1(e0, e1):
+            nc.vector.tensor_tensor(total1[:, e0:e1], up[1][:, e0:e1], rest1[:, e0:e1], ADD)
+            res = at("res1_%d" % e0, [P, e1 - e0], F32, TURNED - 192 + e0)
+            nc.scalar.activation(res[:], total1[:, e0:e1], TANH)
             nc.sync.dma_start(out[P : 2 * P, e0:e1], res[:])
 
-        face1(0)
-        face1(1)
-        finish1(0)
-        face1(2)
-        finish1(1)
-        finish1(2)
+        head1.append(fetch_head(1, 1, OWN0))
+        store0(0, on_scalar)
+        store0(1, on_scalar)
+        nc.vector.tensor_tensor(part1[:], own_acc[1][:], tail1[:], ADD)
+        face_term(1, 0, HALF)
+        add_head1(0)
+        face_term(1, HALF, HALF + P)
+        finish1(0, HALF)
+        face_term(1, HALF + P, S)
+        add_head1(1)
+        finish1(HALF, HALF + P)
+        finish1(HALF + P, S)

@@ -46,19 +46,21 @@ def tile_picked_yhodge_tanh_p_kernel(
             return sbuf(name, shape, dtype) if word is None else at(name, shape, dtype, word)
 
         RAW1 = 0
-        RAW2 = [2 * S, 4 * S]
+        RAW3_FIRST = 4 * S
+        RAW2 = [2 * S, 6 * S]
+        DV1 = RAW2[1] - 192
         LI1 = RAW2[1] + S + 64
         CODES2 = LI1 + S
-        RAW3_FIRST = CODES2 + S
-        RAW3 = RAW3_FIRST + 3 * S
+        RAW3 = CODES2 + 2 * S
         UP0 = RAW3 - S + 64
         CU1 = RAW3 + 64
-        HEAD0 = RAW3 + 384
-        TAIL1 = HEAD0 + S
-        HEAD1 = TAIL1 + S
-        CODES3 = HEAD1 + HALF - 64
+        TAIL1 = RAW3 + 384
+        HEAD0 = RAW3 + 2 * S
+        CODES3 = HEAD0 + HALF - 64
         OWN0 = CODES3 + N
-        TURNED = OWN0 + S + 192
+        RES1 = OWN0 + S
+        TURNED = RES1 + HALF - 64
+        UP1 = RES1 + S
 
         def bank(name, i, width):
             return psum.tile([P, width], F32, name=name, tag="bank%d" % i)
@@ -216,7 +218,7 @@ def tile_picked_yhodge_tanh_p_kernel(
             return li
 
         def node_sum(b, li):
-            win = at("dv_win%d" % b, [P, S + SPARE], F32, (RAW1, RAW2[1])[b])
+            win = at("dv_win%d" % b, [P, S + SPARE], F32, (RAW1, DV1)[b])
             pairs = li[:].rearrange("p (v d) -> p d v", d=2)
             nc.vector.tensor_tensor(win[:, 0:V], pairs[:, 0, :], pairs[:, 1, :], ADD)
             return win
@@ -244,14 +246,14 @@ def tile_picked_yhodge_tanh_p_kernel(
         wq = quantize("q2_1", g2[:, 1], N)
         for o in range(PASSES):
             mx_pass(h1_acc[:], wq, o * P, o, 0, S)
-        dv_win.append(node_sum(1, li1))
 
         own_acc = [bank("own%d" % b, 6 + b, S) for b in range(BLOCKS)]
         sum0 = [bank("sum0%d" % i, (4, 0)[i], HALF) for i in range(2)]
         h_win = [sbuf("h_win0", [P, S], F32), at("h_win1", [P, S], F32, RAW3_FIRST)]
         sides = [sbuf("sides%d" % b, [P, 2 * V], F32) for b in range(BLOCKS)]
         cu_win = [at("cu_win%d" % b, [P, V + SPARE], F32, (RAW3_FIRST + S, CU1)[b]) for b in range(BLOCKS)]
-        up = [at("up0", [P, S], F32, UP0), sbuf("up1", [P, S], F32)]
+        up0 = at("up0", [P, S], F32, UP0)
+        up = [[up0[:, e0:e1] for e0, e1 in halves], []]
 
         def curl_term(b, d):
             signed(sides[b][:, d * V : (d + 1) * V], h_win[b], (tri_t, trj_t)[d], 0, V, (sa_t, sb_t)[d][:])
@@ -259,11 +261,12 @@ def tile_picked_yhodge_tanh_p_kernel(
         def curl_sum(b):
             nc.vector.tensor_tensor(cu_win[b][:, 0:V], sides[b][:, 0:V], sides[b][:, V:], ADD)
 
-        def face_term(b, e0, e1):
-            signed(up[b][:, e0:e1], cu_win[b], face_t, e0, e1, sf_t[:, e0:e1])
+        def face_term(b, i):
+            e0, e1 = halves[i]
+            signed(up[b][i], cu_win[b], face_t, e0, e1, sf_t[:, e0:e1])
 
         def own_passes(o, grouped):
-            wq = quantize("q3_%d" % o, grouped[:], N, ((None, CODES3)[o], None))
+            wq = quantize("q3_%d" % o, grouped[:], N, ((None, None), (CODES3, UP1))[o])
             for b in range(BLOCKS):
                 mx_pass(own_acc[b][:], wq, b * P, o, 0, S)
 
@@ -285,58 +288,64 @@ def tile_picked_yhodge_tanh_p_kernel(
         curl_term(0, 1)
         own_passes(0, g3_0)
         curl_sum(0)
+        dv_win.append(node_sum(1, li1))
         own_passes(1, g3_1)
-        face_term(0, 0, HALF)
+        face_term(0, 0)
         curl_term(1, 0)
         curl_term(1, 1)
-        face_term(0, HALF, S)
+        face_term(0, 1)
         curl_sum(1)
-        head0.append(fetch_head(0, 1, HEAD0))
         tail1 = fetch("tail1", dv_win[1], tail_t, -1.0, TAIL1)
         own0 = at("own0_sb", [P, S], F32, OWN0)
         nc.scalar.copy(own0[:], own_acc[0][:])
-        head1 = [fetch_head(1, 0, HEAD1)]
-        add_turned(sum0[0], up[0][:, 0:HALF])
-        for i in range(2):
-            add_turned(sum0[i], head0[i])
-        add_turned(sum0[1], up[0][:, HALF:])
-        for i, (e0, e1) in enumerate(halves):
-            add_turned(sum0[i], own0[:, e0:e1], last=True)
-        backs = []
-        for i in range(2):
-            turned = at("turned0%d" % i, [P, HALF], F32, (TURNED + 3 * P, TURNED)[i])
-            nc.scalar.activation(turned[:], sum0[i][:], TANH)
-            backs.append(turn_back("back0%d" % i, turned, 1 + i))
+        head0.append(fetch_head(0, 1, HEAD0))
+        add_turned(sum0[0], head0[0])
+        add_turned(sum0[0], up[0][0])
+        add_turned(sum0[0], own0[:, 0:HALF], last=True)
+        add_turned(sum0[1], own0[:, HALF:])
+        add_turned(sum0[1], up[0][1])
+        add_turned(sum0[1], head0[1], last=True)
 
-        def store0(i, copy):
+        def squash(name, acc, i, word=None):
+            turned = place("turned" + name, [P, HALF], F32, word)
+            nc.scalar.activation(turned[:], acc[:], TANH)
+            return turn_back("back" + name, turned, i)
+
+        def store(back, b, i, copy):
             e0, e1 = halves[i]
-            res = sbuf("res0%d" % i, [P, HALF], F32)
-            copy(res[:], backs[i][:])
-            nc.sync.dma_start(out[0:P, e0:e1], res[:])
+            res = sbuf("res%d%d" % (b, i), [P, HALF], F32)
+            copy(res[:], back[:])
+            nc.sync.dma_start(out[b * P : (b + 1) * P, e0:e1], res[:])
 
         part1 = sbuf("part1", [P, S], F32)
         rest1 = sbuf("rest1", [P, S], F32)
         total1 = sbuf("total1", [P, S], F32)
 
-        def add_head1(i):
-            e0, e1 = halves[i]
-            nc.vector.tensor_tensor(rest1[:, e0:e1], part1[:, e0:e1], head1[i][:], ADD)
+        def add_head1(e0, e1):
+            i, c = divmod(e0, HALF)
+            nc.vector.tensor_tensor(rest1[:, e0:e1], part1[:, e0:e1], head1[i][:, c : c + e1 - e0], ADD)
 
         def finish1(e0, e1):
-            nc.vector.tensor_tensor(total1[:, e0:e1], up[1][:, e0:e1], rest1[:, e0:e1], ADD)
-            res = at("res1_%d" % e0, [P, e1 - e0], F32, TURNED - 192 + e0)
+            i, c = divmod(e0, HALF)
+            nc.vector.tensor_tensor(total1[:, e0:e1], up[1][i][:, c : c + e1 - e0], rest1[:, e0:e1], ADD)
+            res = at("res1_%d" % e0, [P, e1 - e0], F32, RES1 + e0)
             nc.scalar.activation(res[:], total1[:, e0:e1], TANH)
             nc.sync.dma_start(out[P : 2 * P, e0:e1], res[:])
 
-        head1.append(fetch_head(1, 1, OWN0))
-        store0(0, on_scalar)
-        store0(1, on_scalar)
+        back00 = squash("00", sum0[0], 1, UP1 + HALF)
+        head1 = [fetch_head(1, 0, OWN0)]
+        back01 = squash("01", sum0[1], 2, TURNED)
+        head1.append(fetch_head(1, 1, HEAD0))
+        store(back00, 0, 0, on_scalar)
+        store(back01, 0, 1, on_scalar)
         nc.vector.tensor_tensor(part1[:], own_acc[1][:], tail1[:], ADD)
-        face_term(1, 0, HALF)
-        add_head1(0)
-        face_term(1, HALF, HALF + P)
+        for i in range(2):
+            up[1].append(at("up1%d" % i, [P, HALF], F32, UP1 + i * HALF)[:])
+        face_term(1, 0)
+        add_head1(0, HALF)
+        face_term(1, 1)
         finish1(0, HALF)
-        face_term(1, HALF + P, S)
-        add_head1(1)
+        add_head1(HALF, HALF + P)
+        add_head1(HALF + P, S)
         finish1(HALF, HALF + P)
         finish1(HALF + P, S)

@@ -197,12 +197,23 @@ def tile_picked_yhodge_tanh_p_kernel(
         for o, b in ((0, 0), (1, 0), (0, 1)):
             g1[o, b] = interleave("g1_%d%d" % (o, b), w1_raw[o, b], P, on_scalar)
 
-        def y_passes(o, b):
+        def y_passes(o, b, warm=False):
             wq = quantize("q1_%d%d" % (o, b), g1[o, b][:], P)
             for i, (e0, e1) in enumerate(halves):
                 mx_pass(y_acc[b][i][:], wq, 0, o, e0, e1)
+            if warm:
+                idle = bank("warm", 7, S)
+                nc.tensor.matmul_mx(
+                    out=idle[:],
+                    lhsT=wq[0][:].bitcast(FP8X4),
+                    lhsT_scale=wq[1][:],
+                    rhs=x_pick[0][:].bitcast(FP8X4),
+                    rhs_scale=scale_pick[:],
+                    start=True,
+                    stop=True,
+                )
 
-        y_passes(0, 0)
+        y_passes(0, 0, warm=True)
         nc.vector.tensor_copy(x_pick[1][:], x_all[1][:].indirect(offs_t[:]))
         y_passes(1, 0)
         g1[1, 1] = interleave("g1_11", w1_raw[1, 1], P, on_vector)

@@ -234,27 +234,32 @@ def tile_picked_yhodge_tanh_p_kernel(
             nc.vector.tensor_tensor(win[:, 0:V], pairs[:, 0, :], pairs[:, 1, :], ADD)
             return win
 
-        g2 = sbuf("g2", [P, BLOCKS, PASSES * P, PACK], BF16)
+        g2 = [sbuf("g2_%d" % b, [P, PASSES * P, PACK], BF16) for b in range(BLOCKS)]
 
-        def interleave_w2(o, copy, b0=0, b1=BLOCKS):
+        def interleave_w2(o, b, copy):
             copy(
-                g2[:, b0:b1, o * P : (o + 1) * P, :].rearrange("p b (c i) t -> p b c t i", i=4),
-                w2_raw[o][:, :, b0 * P : b1 * P].rearrange("p t (b c i) -> p b c t i", b=b1 - b0, i=4),
+                g2[b][:, o * P : (o + 1) * P, :].rearrange("p (c i) t -> p c t i", i=4),
+                w2_raw[o][:, :, b * P : (b + 1) * P].rearrange("p t (c i) -> p c t i", i=4),
             )
 
         h0_acc = [bank("h0%d" % i, (4, 0)[i], HALF) for i in range(2)]
         h1_acc = bank("h1", 5, S)
-        interleave_w2(0, on_scalar)
+
+        def h0_passes(o, word=None):
+            wq = quantize("q2_%d0" % o, g2[0][:, o * P : (o + 1) * P, :], P, (word, None))
+            for i, (e0, e1) in enumerate(halves):
+                mx_pass(h0_acc[i][:], wq, 0, o, e0, e1)
+
+        for b in range(BLOCKS):
+            interleave_w2(0, b, on_scalar)
         li0 = incidence(0)
         dv_win = [node_sum(0, li0)]
+        h0_passes(0)
         for b in range(BLOCKS):
-            interleave_w2(1, on_vector, b, b + 1)
-        wq = quantize("q2_0", g2[:, 0], N, (CODES2, None))
-        for i, (e0, e1) in enumerate(halves):
-            for o in range(PASSES):
-                mx_pass(h0_acc[i][:], wq, o * P, o, e0, e1)
+            interleave_w2(1, b, on_vector)
+        h0_passes(1, CODES2)
         li1 = incidence(1, LI1)
-        wq = quantize("q2_1", g2[:, 1], N)
+        wq = quantize("q2_1", g2[1][:], N)
         for o in range(PASSES):
             mx_pass(h1_acc[:], wq, o * P, o, 0, S)
 

@@ -252,8 +252,13 @@ def tile_picked_yhodge_tanh_p_kernel(
 
         for b in range(BLOCKS):
             interleave_w2(0, b, on_scalar)
-        li0 = incidence(0)
-        dv_win = [node_sum(0, li0)]
+        li0 = sbuf("li0", [P, S], F32)
+        for e0, e1 in halves:
+            signed(li0[:, e0:e1], y_win[0], inc_t, e0, e1, sn_t[:, e0:e1])
+        dv_win = [at("dv_win0", [P, S + SPARE], F32, RAW1)]
+        for e0, e1 in halves:
+            pairs = li0[:, e0:e1].rearrange("p (v d) -> p d v", d=2)
+            nc.vector.tensor_tensor(dv_win[0][:, e0 // 2 : e1 // 2], pairs[:, 0, :], pairs[:, 1, :], ADD)
         h0_passes(0)
         for b in range(BLOCKS):
             interleave_w2(1, b, on_vector)

@@ -57,7 +57,8 @@ def tile_picked_yhodge_tanh_p_kernel(
         TAIL1 = RAW3 + 384
         HEAD0 = RAW3 + 2 * S
         CODES3 = HEAD0 + HALF - 64
-        OWN0 = CODES3 + N
+        HEAD10 = CODES3 + N - 64
+        OWN0 = HEAD10 + HALF
         RES1 = OWN0 + S
         TURNED = RES1 + HALF - 64
         UP1 = RES1 + S
@@ -253,10 +254,11 @@ def tile_picked_yhodge_tanh_p_kernel(
         for b in range(BLOCKS):
             interleave_w2(0, b, on_scalar)
         li0 = sbuf("li0", [P, S], F32)
-        for e0, e1 in halves:
+        pieces = [(0, S - P), (S - P, S)]
+        for e0, e1 in pieces:
             signed(li0[:, e0:e1], y_win[0], inc_t, e0, e1, sn_t[:, e0:e1])
         dv_win = [at("dv_win0", [P, S + SPARE], F32, RAW1)]
-        for e0, e1 in halves:
+        for e0, e1 in pieces:
             pairs = li0[:, e0:e1].rearrange("p (v d) -> p d v", d=2)
             nc.vector.tensor_tensor(dv_win[0][:, e0 // 2 : e1 // 2], pairs[:, 0, :], pairs[:, 1, :], ADD)
         h0_passes(0)
@@ -354,14 +356,14 @@ def tile_picked_yhodge_tanh_p_kernel(
             nc.sync.dma_start(out[P : 2 * P, e0:e1], res[:])
 
         back00 = squash("00", sum0[0], 1, UP1 + HALF)
-        head1 = [fetch_head(1, 0, OWN0)]
+        head1 = [fetch_head(1, 0, HEAD10)]
         back01 = squash("01", sum0[1], 2, TURNED)
         head1.append(fetch_head(1, 1, HEAD0))
         store(back00, 0, 0, on_scalar)
         store(back01, 0, 1, on_scalar)
         nc.vector.tensor_tensor(part1[:], own_acc[1][:], tail1[:], ADD)
         for i in range(2):
-            up[1].append(at("up1%d" % i, [P, HALF], F32, UP1 + i * HALF)[:])
+            up[1].append(at("up1%d" % i, [P, HALF], F32, (UP1, OWN0)[i])[:])
         face_term(1, 0)
         add_head1(0, HALF)
         face_term(1, 1)

from contextlib import ExitStack

import concourse.mybir as mybir
from concourse.masks import make_identity

K, T, S, N, V = 1024, 1024, 512, 256, 256
P = 128
PACK = 4
K_PASS = P * PACK
PASSES = K // K_PASS
BLOCKS = N // P
HALF = S // 2
SPARE = 16
SCALE_ROWS = 4
FLOPS = 3 * 2 * K * N * S

F32 = mybir.dt.float32
BF16 = mybir.dt.bfloat16
I32 = mybir.dt.int32
U32 = mybir.dt.uint32
U16 = mybir.dt.uint16
U8 = mybir.dt.uint8
FP8X4 = mybir.dt.float8_e4m3fn_x4
ADD = mybir.AluOpType.add
MULT = mybir.AluOpType.mult
TANH = mybir.ActivationFunctionType.Tanh
COPY = mybir.ActivationFunctionType.Copy


def tile_picked_yhodge_tanh_p_kernel(
    tc, x_words, x_scales, w1, w2, w3, sn, sa, sb, sf, offs, inc, head, tail, tri, trj, face, out
):
    nc = tc.nc
    with ExitStack() as ctx:
        keep = ctx.enter_context(tc.tile_pool(name="keep", bufs=1))
        shared = ctx.enter_context(tc.tile_pool(name="shared", bufs=1))
        psum = ctx.enter_context(tc.psum_pool(name="psum", bufs=1))

        def sbuf(name, shape, dtype, tag=None):
            return keep.tile(shape, dtype, name=name, tag=tag or name, align_bytes=256)

        def at(name, shape, dtype, word):
            return shared.tile(shape, dtype, name=name, offset=4 * word, align_bytes=256)

        def place(name, shape, dtype, word):
            return sbuf(name, shape, dtype) if word is None else at(name, shape, dtype, word)

        RAW1 = 0
        RAW3_FIRST = 4 * S
        RAW2 = [2 * S, 6 * S]
        DV1 = RAW2[1] - 192
        LI1 = RAW2[1] + S + 64
        CODES2 = LI1 + S
        RAW3 = CODES2 + 2 * S
        UP0 = RAW3 - S + 64
        CU1 = RAW3 + 64
        TAIL1 = RAW3 + 384
        HEAD0 = RAW3 + 2 * S
        CODES3 = HEAD0 + HALF - 64
        HEAD10 = CODES3 + N - 64
        OWN0 = HEAD10 + HALF
        RES1 = OWN0 + S
        TURNED = RES1 + HALF - 64
        UP1 = RES1 + S

        def bank(name, i, width):
            return psum.tile([P, width], F32, name=name, tag="bank%d" % i)

        def load(name, src, dtype):
            t = sbuf(name, list(src.shape), dtype)
            nc.sync.dma_start(t[:], src)
            return t

        def load_words(o):
            t = sbuf("x_all%d" % o, [P, T], U32)
            nc.sync.dma_start(t[:].bitcast(I32), x_words[o].rearrange("p c r -> p (c r)").bitcast(I32))
            return t

        def load_weight(name, w, o, c0=0, width=N, word=None):
            t = place(name, [P, PACK, width], F32, word)
            rows = w[o * K_PASS : (o + 1) * K_PASS, c0 : c0 + width]
            nc.sync.dma_start(t[:], rows.rearrange("(p t) c -> p t c", t=PACK))
            return t

        def window(name, used, width):
            t = sbuf(name, [P, width], F32)
            nc.vector.memset(t[:, used:], 0.0)
            return t

        scale_all = sbuf("scale_all", [P, T], U8)
        nc.gpsimd.memset(scale_all[:].bitcast(I32), 0)
        zeros = sbuf("zeros", [P, SPARE], F32)
        nc.vector.memset(zeros[:], 0.0)
        y_win0 = sbuf("y_win0", [P, S + SPARE], F32)

        x_all = [load_words(0)]
        offs_t = load("offs_t", offs, U16)
        for q in range(4):
            nc.sync.dma_start(
                scale_all[32 * q : 32 * q + PASSES * SCALE_ROWS, :].bitcast(I32),
                x_scales[:, SCALE_ROWS * q : SCALE_ROWS * (q + 1), :].bitcast(I32),
            )
        nc.scalar.activation(y_win0[:, S:], zeros[:], TANH)
        ident = sbuf("ident", [P, P], F32)
        make_identity(nc, ident[:])
        y_win = [y_win0, window("y_win1", S, S + SPARE)]

        w1_raw = {}

        def load_w1(o, b):
            word = RAW1 + o * S if b == 0 else None
            w1_raw[o, b] = load_weight("w1_raw%d%d" % (o, b), w1, o, b * P, P, word)

        load_w1(0, 0)
        x_all.append(load_words(1))
        load_w1(1, 0)
        load_w1(0, 1)
        load_w1(1, 1)
        inc_t = load("inc_t", inc, U16)
        sn_t = load("sn_t", sn, F32)
        w2_raw = [load_weight("w2_raw%d" % o, w2, o, word=RAW2[o]) for o in range(PASSES)]
        tail_t = load("tail_t", tail, U16)
        head_t = load("head_t", head, U16)
        tri_t = load("tri_t", tri, U16)
        trj_t = load("trj_t", trj, U16)
        sa_t = load("sa_t", sa, F32)
        sb_t = load("sb_t", sb, F32)
        w3_raw = [load_weight("w3_raw%d" % o, w3, o, word=(RAW3_FIRST, RAW3)[o]) for o in range(PASSES)]
        face_t = load("face_t", face, U16)
        sf_t = load("sf_t", sf, F32)

        def cols(lst, e0, e1):
            return lst[:, e0 // 16 : e1 // 16]

        halves = [(0, HALF), (HALF, S)]
        x_pick = [sbuf("x_pick%d" % o, [P, S], U32) for o in range(PASSES)]
        scale_pick = sbuf("scale_pick", [P, S], U8)
        nc.vector.tensor_copy(x_pick[0][:], x_all[0][:].indirect(offs_t[:]))
        nc.vector.tensor_copy(scale_pick[:], scale_all[:].indirect(offs_t[:]))

        def interleave(name, raw, width, copy, word=None):
            grouped = place(name, [P, width, PACK], BF16, word)
            copy(
                grouped[:].rearrange("p (c i) t -> p c t i", i=4),
                raw[:].rearrange("p t (c i) -> p c t i", i=4),
            )
            return grouped

        def quantize(name, grouped, width, words=(None, None)):
            codes = place(name + "_codes", [P, width], U32, words[0])
            scales = place(name + "_scales", [P, width], U8, words[1])
            nc.vector.quantize_mx(
                out=codes[:].bitcast(FP8X4), scales=scales[:], in_=grouped.rearrange("p c t -> p (c t)")
            )
            return codes, scales

        def mx_pass(acc, wq, c0, o, e0, e1):
            codes, scales = wq
            nc.tensor.matmul_mx(
                out=acc,
                lhsT=codes[:, c0 : c0 + P].bitcast(FP8X4),
                lhsT_scale=scales[:, c0 : c0 + P],
                rhs=x_pick[o][:, e0:e1].bitcast(FP8X4),
                rhs_scale=scale_pick[SCALE_ROWS * o :, e0:e1],
                start=o == 0,
                stop=o == PASSES - 1,
            )

        def signed(dst, win, lst, e0, e1, sign):
            nc.vector.tensor_tensor(dst, win[:].indirect(cols(lst, e0, e1)), sign, MULT)

        def fetch(name, win, lst, factor, word=None):
            t = place(name, [P, S], F32, word)
            nc.scalar.activation(t[:], win[:].indirect(lst[:]), COPY, scale=factor)
            return t

        def add_turned(acc, term, first=False, last=False):
            for c in range(2):
                nc.tensor.matmul(
                    acc[:, c * P : (c + 1) * P],
                    term[:, c * P : (c + 1) * P],
                    ident[:],
                    start=first and c == 0,
                    stop=last and c == 1,
                    is_transpose=True,
                )

        def turn_back(name, turned, i):
            back = bank(name, i, HALF)
            for c in range(2):
                nc.tensor.transpose(back[:, c * P : (c + 1) * P], turned[:, c * P : (c + 1) * P], ident[:])
            return back

        on_scalar, on_vector = nc.scalar.copy, nc.vector.tensor_copy

        y_acc = [[bank("y%d%d" % (b, i), 2 * b + i, HALF) for i in range(2)] for b in range(BLOCKS)]
        g1 = {}
        for o, b in ((0, 0), (1, 0), (0, 1)):
            g1[o, b] = interleave("g1_%d%d" % (o, b), w1_raw[o, b], P, on_scalar)

        def y_passes(o, b, warm=False):
            wq = quantize("q1_%d%d" % (o, b), g1[o, b][:], P)
            for i, (e0, e1) in enumerate(halves):
                mx_pass(y_acc[b][i][:], wq, 0, o, e0, e1)
            if warm:
                idle = bank("warm", 7, S)
                nc.tensor.matmul_mx(
                    out=idle[:],
                    lhsT=wq[0][:].bitcast(FP8X4),
                    lhsT_scale=wq[1][:],
                    rhs=x_pick[0][:].bitcast(FP8X4),
                    rhs_scale=scale_pick[:],
                    start=True,
                    stop=True,
                )

        y_passes(0, 0, warm=True)
        nc.vector.tensor_copy(x_pick[1][:], x_all[1][:].indirect(offs_t[:]))
        y_passes(1, 0)
        g1[1, 1] = interleave("g1_11", w1_raw[1, 1], P, on_vector)
        y_passes(0, 1)
        y_passes(1, 1)
        for b in range(BLOCKS):
            for i, (e0, e1) in enumerate(halves):
                nc.scalar.copy(y_win[b][:, e0:e1], y_acc[b][i][:])

        def incidence(b, word=None):
            li = place("li%d" % b, [P, S], F32, word)
            signed(li[:], y_win[b], inc_t, 0, S, sn_t[:])
            return li

        def node_sum(b, li):
            win = at("dv_win%d" % b, [P, S + SPARE], F32, (RAW1, DV1)[b])
            pairs = li[:].rearrange("p (v d) -> p d v", d=2)
            nc.vector.tensor_tensor(win[:, 0:V], pairs[:, 0, :], pairs[:, 1, :], ADD)
            return win

        g2 = [sbuf("g2_%d" % b, [P, PASSES * P, PACK], BF16) for b in range(BLOCKS)]

        def interleave_w2(o, b, copy):
            copy(
                g2[b][:, o * P : (o + 1) * P, :].rearrange("p (c i) t -> p c t i", i=4),
                w2_raw[o][:, :, b * P : (b + 1) * P].rearrange("p t (c i) -> p c t i", i=4),
            )

        h0_acc = [bank("h0%d" % i, (4, 0)[i], HALF) for i in range(2)]
        h1_acc = bank("h1", 5, S)

        def h0_passes(o, word=None):
            wq = quantize("q2_%d0" % o, g2[0][:, o * P : (o + 1) * P, :], P, (word, None))
            for i, (e0, e1) in enumerate(halves):
                mx_pass(h0_acc[i][:], wq, 0, o, e0, e1)

        for b in range(BLOCKS):
            interleave_w2(0, b, on_scalar)
        li0 = sbuf("li0", [P, S], F32)
        pieces = [(0, S - P), (S - P, S)]
        for e0, e1 in pieces:
            signed(li0[:, e0:e1], y_win[0], inc_t, e0, e1, sn_t[:, e0:e1])
        dv_win = [at("dv_win0", [P, S + SPARE], F32, RAW1)]
        for e0, e1 in pieces:
            pairs = li0[:, e0:e1].rearrange("p (v d) -> p d v", d=2)
            nc.vector.tensor_tensor(dv_win[0][:, e0 // 2 : e1 // 2], pairs[:, 0, :], pairs[:, 1, :], ADD)
        h0_passes(0)
        for b in range(BLOCKS):
            interleave_w2(1, b, on_vector)
        h0_passes(1, CODES2)
        li1 = incidence(1, LI1)
        wq = quantize("q2_1", g2[1][:], N)
        for o in range(PASSES):
            mx_pass(h1_acc[:], wq, o * P, o, 0, S)

        own_acc = [bank("own%d" % b, 6 + b, S) for b in range(BLOCKS)]
        sum0 = [bank("sum0%d" % i, (4, 0)[i], HALF) for i in range(2)]
        h_win = [sbuf("h_win0", [P, S], F32), at("h_win1", [P, S], F32, RAW3_FIRST)]
        sides = [sbuf("sides%d" % b, [P, 2 * V], F32) for b in range(BLOCKS)]
        cu_win = [at("cu_win%d" % b, [P, V + SPARE], F32, (RAW3_FIRST + S, CU1)[b]) for b in range(BLOCKS)]
        up0 = at("up0", [P, S], F32, UP0)
        up = [[up0[:, e0:e1] for e0, e1 in halves], []]

        def curl_term(b, d):
            signed(sides[b][:, d * V : (d + 1) * V], h_win[b], (tri_t, trj_t)[d], 0, V, (sa_t, sb_t)[d][:])

        def curl_sum(b):
            nc.vector.tensor_tensor(cu_win[b][:, 0:V], sides[b][:, 0:V], sides[b][:, V:], ADD)

        def face_term(b, i):
            e0, e1 = halves[i]
            signed(up[b][i], cu_win[b], face_t, e0, e1, sf_t[:, e0:e1])

        def own_passes(o, grouped):
            wq = quantize("q3_%d" % o, grouped[:], N, ((None, None), (CODES3, UP1))[o])
            for b in range(BLOCKS):
                mx_pass(own_acc[b][:], wq, b * P, o, 0, S)

        def fetch_head(b, i, word):
            t = place("head%d%d" % (b, i), [P, HALF], F32, word)
            nc.scalar.activation(t[:], dv_win[b][:].indirect(cols(head_t, *halves[i])), COPY)
            return t

        tail0 = fetch("tail0", dv_win[0], tail_t, -1.0)
        head0 = [fetch_head(0, 0, None)]
        for i, (e0, e1) in enumerate(halves):
            nc.scalar.copy(h_win[0][:, e0:e1], h0_acc[i][:])
        for i, (e0, e1) in enumerate(halves):
            add_turned(sum0[i], tail0[:, e0:e1], first=True)
        g3_0 = interleave("g3_0", w3_raw[0], N, on_scalar, CODES2)
        g3_1 = interleave("g3_1", w3_raw[1], N, on_scalar)
        nc.scalar.copy(h_win[1][:], h1_acc[:])
        curl_term(0, 0)
        curl_term(0, 1)
        own_passes(0, g3_0)
        curl_sum(0)
        dv_win.append(node_sum(1, li1))
        own_passes(1, g3_1)
        face_term(0, 0)
        curl_term(1, 0)
        curl_term(1, 1)
        face_term(0, 1)
        curl_sum(1)
        tail1 = fetch("tail1", dv_win[1], tail_t, -1.0, TAIL1)
        own0 = at("own0_sb", [P, S], F32, OWN0)
        nc.scalar.copy(own0[:], own_acc[0][:])
        head0.append(fetch_head(0, 1, HEAD0))
        add_turned(sum0[0], head0[0])
        add_turned(sum0[0], up[0][0])
        add_turned(sum0[0], own0[:, 0:HALF], last=True)
        add_turned(sum0[1], own0[:, HALF:])
        add_turned(sum0[1], up[0][1])
        add_turned(sum0[1], head0[1], last=True)

        def squash(name, acc, i, word=None):
            turned = place("turned" + name, [P, HALF], F32, word)
            nc.scalar.activation(turned[:], acc[:], TANH)
            return turn_back("back" + name, turned, i)

        def store(back, b, i, copy):
            e0, e1 = halves[i]
            res = sbuf("res%d%d" % (b, i), [P, HALF], F32)
            copy(res[:], back[:])
            nc.sync.dma_start(out[b * P : (b + 1) * P, e0:e1], res[:])

        part1 = sbuf("part1", [P, S], F32)
        rest1 = sbuf("rest1", [P, S], F32)
        total1 = sbuf("total1", [P, S], F32)

        def add_head1(e0, e1):
            i, c = divmod(e0, HALF)
            nc.vector.tensor_tensor(rest1[:, e0:e1], part1[:, e0:e1], head1[i][:, c : c + e1 - e0], ADD)

        def finish1(e0, e1):
            i, c = divmod(e0, HALF)
            nc.vector.tensor_tensor(total1[:, e0:e1], up[1][i][:, c : c + e1 - e0], rest1[:, e0:e1], ADD)
            res = at("res1_%d" % e0, [P, e1 - e0], F32, RES1 + e0)
            nc.scalar.activation(res[:], total1[:, e0:e1], TANH)
            nc.sync.dma_start(out[P : 2 * P, e0:e1], res[:])

        back00 = squash("00", sum0[0], 1, UP1 + HALF)
        head1 = [fetch_head(1, 0, HEAD10)]
        back01 = squash("01", sum0[1], 2, TURNED)
        head1.append(fetch_head(1, 1, HEAD0))
        store(back00, 0, 0, on_scalar)
        store(back01, 0, 1, on_scalar)
        nc.vector.tensor_tensor(part1[:], own_acc[1][:], tail1[:], ADD)
        for i in range(2):
            up[1].append(at("up1%d" % i, [P, HALF], F32, (UP1, OWN0)[i])[:])
        face_term(1, 0)
        add_head1(0, HALF)
        face_term(1, 1)
        finish1(0, HALF)
        add_head1(HALF, HALF + P)
        add_head1(HALF + P, S)
        finish1(HALF, HALF + P)
        finish1(HALF + P, S)
